import numpy as np, ml_dtypes
CORES = [40,41,42,43,44,45,46,47]
N = 8
BF = ml_dtypes.bfloat16
def gentries(a):
    return np.ascontiguousarray(a.reshape(8, 16, -1).transpose(0, 2, 1)).reshape(8, -1)
def gtable(e):
    e = np.asarray(e); return np.ascontiguousarray(e.reshape(8, -1, 16).transpose(0, 2, 1)).reshape(128, -1).astype(np.int32)
V, D, L, CAP, RO = 2048, 7, 3, 128, 2
K = V // 256
def pack(w, z, cd):
    return {"wish": np.ascontiguousarray(w.reshape(N, 128, V)).astype(np.float32).astype(BF), "goods": np.ascontiguousarray(z.reshape(N, 128, V)).astype(np.float32).astype(BF),
            "cand": np.stack([gtable(a.reshape(8, -1)) for a in cd])}
def ring(o, m):
    a = o[:len(o) // m * m].reshape(-1, m)
    return a, np.roll(a, -1, axis=1)
def lead(rng, w, z, cd, q, g, a, b):
    w[q, g][:, a] = z[q, g][:, b]; cd[q, g][rng.integers(0, D, a.shape), a] = b
def coded(rng):
    h = rng.integers(0, 256, (N, 8, 8, V)); n = np.argsort(rng.random((N, 8, V)), axis=-1)
    h[:, :, 0] = n & 255; h[:, :, 1] = n >> 8
    return np.concatenate([h, 255 - h], axis=2)
def part(rng, z):
    return (z * rng.random(z.shape)).astype(np.int64)
def twice(rng, w, z, cd, q, g, o):
    a, b = ring(o, L); n = len(a); x = np.arange(n)[:, None]; j = np.arange(L)[None, :]
    c = np.argsort(rng.random((n, 16)), axis=1)[:, :L]
    lo = rng.integers(0, 2, (n, L)); st = np.where(rng.random((n, 1, 1)) < 0.5, 1, rng.integers(1, 127, (n, L, 2)))
    zz = rng.integers(0, 4, (n, 1, 16)) + np.zeros((n, L, 16), np.int64); ww = np.full((n, L, 16), 255)
    for k in range(L):
        zz[x, (j + k) % L, c] = (lo, lo + st[:, :, 0], lo + st[:, :, 0] + st[:, :, 1])[k] if k < 3 else lo
        if k: ww[x, (j + k) % L, c] = 0
    z[q, g][:, a] = zz.transpose(2, 0, 1); w[q, g][:, a] = ww.transpose(2, 0, 1)
    cd[q, g][:, a] = np.where(rng.random((D,) + a.shape) < 0.5, a, b); cd[q, g][rng.integers(0, D, a.shape), a] = b
def calm(rng, w, z, cd, g):
    sets = []
    for q in range(N):
        o = rng.permutation(V); n = int(rng.integers(2, CAP + 1))
        sets.append((n, np.concatenate([np.sort(o[:n]), np.sort(o[n:])])))
    for q in range(N):
        n, s = sets[q]; k = s[:CAP]; come = z[q - 1, g][:, sets[q - 1][1][:CAP]]
        w[q, g][:, k] = part(rng, np.minimum(z[q, g][:, k], come)); w[q, g][:, s[:n]] = come[:, :n]
        v = rng.permutation(s[CAP:])[:n]
        z[q, g][:, v] = come[:, :n]; w[q, g][:, v] = part(rng, come[:, :n])
        cd[q, g][rng.integers(0, D, n), s[:n]] = v
def plant(rng, w, z, cd):
    for q in range(N):
        share = rng.permutation(np.array([0.01, 0.05, 0.3, 0.9, 0.01, 0.1, 0.5, 0.9]))
        for g in range(8):
            o = rng.permutation(V); i = 0
            for m in range(2, L + 2):
                a, b = ring(o[i:i + m * K], m); i += m * K
                lead(rng, w, z, cd, q, g, a, b)
                w[q, g][:, a] = np.clip(w[q, g][:, a] + rng.integers(-3, 2, (16,) + a.shape), 0, 255)
            p = o[i:i + RO * K].reshape(RO, K); i += RO * K
            u = o[i:i + RO * K].reshape(RO, K); i += RO * K
            for j in range(RO):
                s = rng.permutation(D); v = u[max(j - 1, 0)]
                if j: z[q, g][:, u[j]] = np.maximum(z[q, g][:, v] - rng.integers(0, 4, (16, K)), 0)
                w[q, g][:, p[j]] = z[q, g][:, v]; w[q, g][:, u[j]] = z[q, g][:, p[j]]
                cd[q, g][s[0], p[j]] = v; cd[q, g][s[1], p[j]] = u[j]; cd[q, g][s[2], u[j]] = p[j]
            r = o[i:]; r = r[rng.random(len(r)) >= share[g]]
            w[q, g][:, r] = part(rng, z[q, g][:, r])
    return pack(w, z, cd)
def setup_inputs(rng):
    z = rng.integers(0, 256, (N, 8, 16, V)); w = rng.integers(0, 256, (N, 8, 16, V)); cd = rng.integers(0, V, (N, 8, D, V))
    return plant(rng, w, z, cd)
def setup_inputs_room(rng):
    z = coded(rng); w = part(rng, z); cd = rng.integers(0, V, (N, 8, D, V))
    for q in range(N):
        for g in range(8):
            n = int(rng.choice(np.array([0, 1, CAP - 1, CAP, CAP + 1, V // 2])))
            if q < 2: n = (CAP, CAP + 1, CAP - 1, 1, 0, V // 2, CAP, CAP + 1)[(g + q) % 8]
            o = rng.permutation(V); i = n
            if q < 2 and n:
                j = int(np.flatnonzero(o == V - 1)[0]); o[j] = o[0]; o[0] = V - 1
            lead(rng, w, z, cd, q, g, o[:n], rng.choice(o[n:], n))
            for m in range(2, L + 1):
                a, b = ring(o[i:i + m * K], m); i += m * K
                lead(rng, w, z, cd, q, g, a, b)
    return pack(w, z, cd)
def setup_inputs_rings(rng):
    z = coded(rng); w = part(rng, z); cd = rng.integers(0, V, (N, 8, D, V)); far = int(np.lcm.reduce(np.arange(1, L + 1)))
    calm(rng, w, z, cd, 5)
    for q in range(N):
        for g in range(8):
            if g == 5: continue
            if g == 4:
                w[q, g][:, :CAP] = 0
                twice(rng, w, z, cd, q, g, CAP + rng.permutation(V - CAP)); continue
            ms = [[L + 1], [2], [3], [L]][g] if g < 4 else [int(m) for m in rng.permutation(np.array(list(range(1, L + 3)) + [2 * L, 3 * L, far]))]
            o = rng.permutation(V); n = V // sum(ms); i = 0
            for m in ms:
                a, b = ring(o[i:i + n * m], m); i += n * m
                lead(rng, w, z, cd, q, g, a, b)
            if i < V:
                a, b = ring(o[i:], V - i); lead(rng, w, z, cd, q, g, a, b)
    return pack(w, z, cd)
def setup_inputs_ties(rng):
    z = np.zeros((N, 8, 16, V), np.int64); w = np.zeros((N, 8, 16, V), np.int64); cd = np.zeros((N, 8, D, V), np.int64); h = V // 2; t = V // 4
    for q in range(N):
        for g in range(8):
            o = rng.permutation(V); lo, hi = o[:h], o[h:]
            bl = np.concatenate([rng.integers(0, 61, 12), np.full(4, 255)]); bh = rng.integers(150, 255, 16)
            tl = np.stack([rng.permutation(bl) for _ in range(5)], axis=1); th = np.stack([rng.permutation(bh) for _ in range(5)], axis=1)
            zz, ww, cc = z[q, g], w[q, g], cd[q, g]
            zz[:, lo] = tl[:, rng.integers(0, 5, h)]; zz[:, hi] = th[:, rng.integers(0, 5, h)]
            cc[:, :] = rng.choice(lo, (D, V))
            a, b = lo[:t], hi[:t]; three = rng.random(t) < 0.5
            ww[:, a] = 255; ww[:, b] = zz[:, a]; cc[0, b] = a
            cc[D - 1, a] = np.where(rng.random(t) < 0.5, a, cc[D - 1, a])
            p = np.argsort(rng.random((t, D)), axis=1); x = np.sort(p[:, :3], axis=1); x2 = np.sort(p[:, :2], axis=1)
            x[~three] = x2[~three][:, [0, 1, 1]]
            which = np.where(three, rng.integers(0, 3, t), rng.integers(0, 2, t))
            v = np.where(np.arange(3)[:, None] == which[None, :], b[None, :], rng.choice(hi, (3, t))); v[2] = np.where(three, v[2], v[1])
            for i in range(3): cc[x[:, i], a] = v[i]
            e = hi[t:]; ww[:, e] = 255; cc[:, e] = np.roll(e.reshape(-1, 2), 1, axis=1).reshape(-1)[None, :]
            c = lo[t:]; ww[:, c] = np.concatenate([tl, th], axis=1)[:, rng.integers(0, 10, len(c))]
            cc[:, c] = rng.integers(0, V, (D, len(c))); cc[0, c] = np.where(rng.random(len(c)) < 0.3, c, cc[0, c]); cc[2, c] = np.where(rng.random(len(c)) < 0.5, cc[0, c], cc[2, c])
    return pack(w, z, cd)
def setup_inputs_ends(rng):
    z = rng.integers(0, 256, (N, 8, 16, V)); w = rng.integers(0, 256, (N, 8, 16, V)); cd = rng.integers(0, V, (N, 8, D, V))
    cd[:, ::2] = rng.choice(np.array([0, V - 1, V // 2, 3]), (N, 4, D, V))
    m = np.arange(V) ^ 1; m = np.where(rng.random(V) < 0.5, m, m[::-1])
    cd[:, 1::2, D - 1] = m; w[:, 1::2] = z[:, 1::2][:, :, :, m]
    w[:, 3::4] = part(rng, z[:, 3::4])
    w[:, 3::4, :, V - 1 - CAP // 2:V - 1] = z[:, 3::4, :, V // 2:V // 2 + 1]; cd[:, 3::4, 1, V - 1 - CAP // 2:V - 1] = V // 2
    w[..., 0] = z[..., V - 1]; w[..., V - 1] = z[..., 0]; cd[:, :, 0, 0] = V - 1; cd[:, :, 0, V - 1] = 0
    return pack(w, z, cd)
def setup_inputs_spread(rng):
    z = np.minimum((np.exp2(8 * rng.random((N, 8, 1, V))) * rng.random((N, 8, 16, V))).astype(np.int64), 255)
    w = np.minimum((np.exp2(8 * rng.random((N, 8, 1, V))) * rng.random((N, 8, 16, V))).astype(np.int64), 255)
    return plant(rng, w, z, rng.integers(0, V, (N, 8, D, V)))
def check_inputs(d):
    bad = []
    for k in ("wish", "goods"):
        v = d[k].astype(np.float32)
        if not np.all((v >= 0) & (v <= 255) & (v == np.floor(v))): bad.append("values of " + k)
    if np.min(d["cand"]) < 0 or np.max(d["cand"]) > V - 1: bad.append("range of cand")
    return bad
def reference(wish, goods, cand):
    w = wish.astype(np.float32).astype(np.int32).reshape(N, 8, 16, V); z = goods.astype(np.float32).astype(np.int32).reshape(N, 8, 16, V)
    cd = np.stack([gentries(a) for a in cand]).astype(np.int64).reshape(N, 8, D, V)
    own = np.zeros((N, 8, V), np.int64) + np.arange(V)
    for t in range(RO):
        best = np.add.reduce(np.maximum(w - z, 0), axis=2); f = own
        for d in range(D):
            c = cd[:, :, d]; s = np.add.reduce(np.maximum(w - np.take_along_axis(z, c[:, :, None, :], 3), 0), axis=2)
            f = np.where(s < best, c, f); best = np.minimum(s, best)
        h = f; back = np.zeros((N, 8, V), bool)
        for i in range(2, L + 1):
            h = np.take_along_axis(f, h, 2); back = back | (h == own)
        trade = (f != own) & back; unmet = (f != own) & ~back
        z = np.take_along_axis(z, np.where(trade, f, own)[:, :, None, :], 3)
        order = np.argsort(~unmet, axis=2, kind="stable")[:, :, None, :CAP]
        away = np.take_along_axis(z, order, 3)
        np.put_along_axis(z, np.broadcast_to(order, (N, 8, 16, CAP)), np.roll(away, 1 + t, axis=0), 3)
    return {"y": z.reshape(N, 128, V).astype(np.float32).astype(BF)}

@@ -1,0 +1,437 @@
+from concourse.bass import DstId, RemoteDMATransfer
+from concourse.mybir import AluOpType as ALU, AxisListType, ActivationFunctionType as ACT
+
+V = 2048
+NB = 136
+ROUNDS = 2
+TRADE_SPLIT = 768
+BF, F32, I32, U16, F16 = "bfloat16", "float32", "int32", "uint16", "float16"
+
+SCRATCH = {}
+for _dt, _bufs in (
+        (BF, "z0 2176 z1 2176 w 2048 mv0 2048 mv1 2048 ms0 2048 ms1 2048 zc 3072 ze0 2048 ze1 2048 eo0 2048 eo1 2048 "
+             "ee0 2048 ee1 2048 win 2048 f1 2048 f2 2048 hlb 256 one 144 ids 640 i4k 128 bo 128 up 128 rw 16 sel 16 "
+             "zj 144 cb 512 eq 256 u 136 s 136 junk 1088 le 288 oh 128 cbf 8 out0 128 out1 128 land0 128 land1 128"),
+        (F16, "c16 1024 cp16 128 i16 128 nw16 128 wt16 128"),
+        (F32, "rcol 8 a16 128 at 128 thr 136 kcol 8 krow 128 bf 128 rf 128 dd 128 cnt 8 pp 136 tm 128 tv 128"),
+        (I32, "ci 896 hl 256 aturn 256 pcol 8 bk 128 rk0 128 rk1 128 rin0 128 rin1 128 oi 16"),
+        (U16, "cu 896 off 256 offc 8 offt 8 offo 8 offg 128")):
+    _w = _bufs.split()
+    for _k in range(0, len(_w), 2):
+        SCRATCH[_w[_k]] = ("sbuf", [128, int(_w[_k + 1])], _dt)
+SCRATCH["xw"] = ("sbuf", [128, 8, 16, 16], BF)
+PSUM = ["d0", "d1", "d2", "k0", "k1", "k2", "k3", "k4"]
+for _k in PSUM:
+    SCRATCH[_k] = ("psum", [128, 512], F32)
+
+LEFT = ["l%d" % _k for _k in range(11)]
+SEMAPHORES = ["eV", "eS", "eP", "eG", "ldca", "ldcb", "ldz", "ldw0", "ldw1", "ldw2", "st", "arr0", "arr1", "pc",
+              "po0", "po1", "pe0", "pe1", "pr0", "pr1"] + LEFT
+
+LISTS = {1: ("V", 0, "k0"), 2: ("V", 1, "k1"), "own": ("E", 0, "k2"), 0: ("E", 1, "k3"), 3: ("S", 2, "k4"),
+         4: ("V", 3, "k0"), 5: ("S", 2, "k1"), 6: ("V", 3, "k2")}
+
+
+def arrange(fixed, free, known):
+    done = dict(known)
+    clock = {e: 0.0 for e in list(fixed) + ["P"]}
+    pos = {e: 0 for e in fixed}
+    free = list(free)
+    out = []
+    while free or any(pos[e] < len(fixed[e]) for e in fixed):
+        cands = []
+        for e in fixed:
+            if pos[e] < len(fixed[e]):
+                t = fixed[e][pos[e]]
+                if all(n in done for n in t[1]):
+                    cands.append((max([clock[e]] + [done[n] for n in t[1]]), 1, e, t))
+        for i, t in enumerate(free):
+            if all(n in done for n in t[1]):
+                cands.append((max([clock["P"]] + [done[n] for n in t[1]]), 0, i, t))
+        start, kind, who, t = min(cands, key=lambda c: (c[0], c[1], str(c[2]).rjust(4)))
+        e = who if kind else "P"
+        if kind:
+            pos[e] += 1
+        else:
+            free.pop(who)
+        clock[e] = start + t[0]
+        done[t[3]] = clock[e] + (t[4] if len(t) > 4 else 0.05)
+        out.append(t[2])
+    return out
+
+
+def rank_program(g, core, T, topo):
+    rank = T.rank_of(core)
+    if rank is None:
+        return
+    n_ranks = len(T.cores)
+    by_die = sorted(T.cores, key=lambda c: (topo.chip(c), topo.die(c), c))
+    place = by_die.index(core)
+    partner = by_die[place + 1 if place % 2 == 0 else place - 1]
+    queue = {"V": g.vector, "S": g.scalar, "P": g.tensor, "G": g, "Y": g.sync}
+    ops, left = [], []
+    pool = (None, "pool", 0, 1)
+
+    def A(name, lo=0, hi=None, step=1, rows=None):
+        hi = SCRATCH[name][1][1] if hi is None else hi
+        r = slice(0, 128) if rows is None else slice(rows[0], rows[1])
+        ap = T[name][r, lo:hi:step] if step > 1 else T[name][r, lo:hi]
+        return (ap, name, lo, hi)
+
+    def op(eng, fn, reads, writes, sem=None, pre=None):
+        ops.append({"eng": eng, "fn": fn, "r": [a[1:] for a in reads], "w": [a[1:] for a in writes], "sem": sem, "pre": pre})
+
+    def ind(win, off):
+        return win[0].indirect(off[0])
+
+    def mm(out, lhs, rhs, start, stop, pre=None):
+        op("P", lambda q: q.matmul(out[0], lhs[0], rhs[0], start, stop), [lhs, rhs], [out], pre=pre)
+
+    def copy(out, in_):
+        op("V", lambda q: q.tensor_copy(out[0], in_[0]), [in_], [out])
+
+    def tt(out, a, b, alu, pre=None):
+        op("V", lambda q: q.tensor_tensor(out[0], a[0], b[0], alu), [a, b], [out], pre=pre)
+
+    def ts(out, a, s1, s2, op0, op1=None):
+        rd = [a] + [s for s in (s1, s2) if isinstance(s, tuple)]
+        v1 = s1[0] if isinstance(s1, tuple) else s1
+        if op1 is None:
+            op("V", lambda q: q.tensor_scalar(out[0], a[0], v1, None, op0), rd, [out])
+        else:
+            op("V", lambda q: q.tensor_scalar(out[0], a[0], v1, s2, op0, op1), rd, [out])
+
+    def gtt(out, win, off, b, alu):
+        op("V", lambda q: q.tensor_tensor(out[0], ind(win, off), b[0], alu), [win, off, b], [out])
+
+    def gather(eng, out, win, off):
+        if eng == "V":
+            op("V", lambda q: q.tensor_copy(out[0], ind(win, off)), [win, off], [out])
+        else:
+            op("S", lambda q: q.activation(out[0], ind(win, off), ACT.Copy), [win, off], [out])
+
+    def act(out, in_, func, scale=1.0, bias=None):
+        if bias is None:
+            op("S", lambda q: q.activation(out[0], in_[0], func, scale=scale), [in_], [out])
+        else:
+            op("S", lambda q: q.activation(out[0], in_[0], func, bias=bias[0], scale=scale), [in_, bias], [out])
+
+    def memset(out, val):
+        op("V", lambda q: q.memset(out[0], val), [], [out])
+
+    def iota(out, pattern, base, mult, whole=False):
+        if whole:
+            op("G", lambda q: q.iota(out[0], pattern, base, mult), [], [out, pool])
+        else:
+            op("G", lambda q: q.iota(out[0], pattern, base, mult, allow_small_or_imprecise_dtypes=True), [], [out, pool])
+
+    def select(out, in_, pattern, cmp, base, mult):
+        op("G", lambda q: q.affine_select(out[0], in_[0], pattern, cmp, 0.0, base, mult), [in_], [out, pool])
+
+    def load(eng, out, src, sem):
+        op(eng, lambda q: q.dma_start(out[0], src), [], [out], sem=(sem, 16))
+
+    def send(dst, land, srcs, sem):
+        rid, pid, _ = topo.addr(dst)
+        mask = topo.mask(core, dst)
+        loc = LEFT[len(left)]
+        left.append((loc, len(topo.engines(core, dst))))
+        if len(srcs) == 1:
+            fn = lambda q: q.remote_dma(land[0], srcs[0][0], T.sem[sem], T.sem[loc], pid, rid, mask)
+        else:
+            fn = lambda q: q.remote_dma_fused(
+                [RemoteDMATransfer(dst_ids=[DstId(rid=rid, pnc=pid)], dma_engine_mask=mask, remote_sem=T.sem[sem],
+                                   srcs=[s[0] for s in srcs], dsts=[land[0]], alu_op=3)], local_sem=T.sem[loc])
+        op("G", fn, srcs, [], sem=left[-1] + ("remote",))
+
+    def xrow(q):
+        return (T.xw[:, :, q, :], "xw", q, q + 1)
+
+    def split(src, first):
+        ts(A("hl", 0, 128), src, 4, 127, ALU.arith_shift_right, ALU.bitwise_and)
+        ts(A("hl", 128, 256), src, 15, None, ALU.bitwise_and)
+        copy(A("hlb"), A("hl"))
+        act(xrow(first + 1), A("hlb", 128, 256), ACT.Copy)
+        copy(xrow(first), A("hlb", 0, 128))
+
+    eye, neye = A("ids", 128, 256), A("ids", 512, 640)
+    from_partner = len(topo.engines(partner, core))
+
+    load("S", A("ci", 0, 256), T.cand[:, 0:256], "ldca")
+    load("Y", A("z0", 0, V), T.goods[:], "ldz")
+    load("Y", A("w", 0, 512), T.wish[:, 0:512], "ldw0")
+    load("Y", A("w", 512, 1024), T.wish[:, 512:1024], "ldw1")
+    load("Y", A("ci", 256, 896), T.cand[:, 256:896], "ldcb")
+    load("Y", A("w", 1024, V), T.wish[:, 1024:V], "ldw2")
+
+    cb_hi = (T.cb[32:64, :], "cb_hi", 0, 512)
+    memset((T.xw[:], "xw", 0, 16), 0.0)
+    memset(cb_hi, float(1 << 19))
+    memset((T.cb[32:64, 256:384], "cb_hi", 256, 384), 0.0)
+    memset(A("le"), -float(NB))
+    iota(A("one"), [[0, 144]], 1, 0)
+    select(eye, A("one", 0, 128), [[-1, 128]], ALU.is_equal, 0, 1)
+    select(A("bo"), A("one", 0, 128), [[-16, 8], [0, 16]], ALU.is_ge, 0, 1)
+    select(A("bo"), A("bo"), [[16, 8], [0, 16]], ALU.is_ge, 15, -1)
+    iota(A("pcol", 0, 1), [[0, 1]], 0, 1, whole=True)
+    iota(A("a16"), [[16, 128]], 0, 0)
+    iota(A("aturn"), [[0, 16], [1, 16]], 0, 16, whole=True)
+    select(A("up"), A("bo"), [[-1, 128]], ALU.is_gt, 0, 1)
+    act(neye, eye, ACT.Copy, -1.0)
+    act(A("ids", 0, 128), eye, ACT.Copy, 16.0)
+    act(A("ids", 256, 384), eye, ACT.Copy, 128.0)
+    act(A("ids", 384, 512), eye, ACT.Copy, 1.0)
+    act(A("i4k"), eye, ACT.Copy, 4096.0)
+    act(A("rw", 0, 8), A("bo", 0, 128, 16), ACT.Copy, -8192.0)
+    act(A("rw", 8, 16), A("bo", 0, 128, 16), ACT.Copy, 8192.0)
+    ts(A("zj"), A("one"), 0.0, None, ALU.mult)
+    copy(A("i16"), eye)
+    ts(A("nw16"), eye, -8192.0, None, ALU.mult)
+    ts(A("pcol", 2, 3), A("pcol", 0, 1), 15, None, ALU.bitwise_and)
+    copy(A("rcol", 0, 1), A("pcol", 2, 3))
+    copy(A("cu", 0, 256), A("ci", 0, 256))
+    copy(A("c16", 0, 256), A("ci", 0, 256))
+    send(partner, A("cp16"), [A("c16", 0, 128)], "pc")
+    iota(A("cb", rows=(0, 32)), [[64, 4], [0, 128]], -256, 0)
+    iota(A("krow"), [[1, 128]], 4097, 0)
+    iota(A("thr", 0, 128), [[0, 128]], 1, 0)
+    iota(A("thr", 128, NB), [[0, 8]], 0, 0)
+    ts(A("zj", 15, 128, 16), A("bo", 0, 128, 16), A("rcol", 0, 1), None, ALU.mult)
+    tt(A("sel", 0, 8), A("ids", 0, 128, 16), A("ids", 129, 256, 16), ALU.add)
+    tt(A("sel", 8, 16), A("ids", 2, 128, 16), A("ids", 131, 256, 16), ALU.add)
+    act(A("at"), A("a16"), ACT.Identity, 1.0, A("rcol", 0, 1))
+    split(A("aturn", 0, 128), 2)
+    copy(A("c16", 896, 1024), A("at"))
+    ts(A("kcol"), A("at", 0, 8), 0.5, None, ALU.add)
+    tt(A("up"), A("i4k"), A("up"), ALU.subtract)
+
+    def pointers(t, z):
+        GV, GS, RELU, MERGE = 3.4, 1.75, 0.6, 0.2
+        z = A(z, 0, V)
+        vq, sq, pq, gq = [], [], [], []
+        if t == 0:
+            known = {"w0": 0.5, "w1": 1.0, "cin": 2.3, "w2": 3.3}
+        else:
+            known = {"w0": 0.0, "w1": 0.0, "w2": 0.0, "cb": 0.0, "cb16": 0.0, "wt": 0.0}
+        part = lambda col: "w%d" % min(col // 512, 2)
+        mbuf = {1: "mv0", 2: "mv1", 4: "mv0", 6: "mv1", 3: "ms0", 5: "ms1", "own": "eo%d" % t, 0: "ee%d" % t}
+        ze, rk, rin = "ze%d" % t, A("rk%d" % t), A("rin%d" % t)
+        offs = lambda d, lo, hi: A("cu", 128 * d + lo // 16, 128 * d + hi // 16)
+        key = lambda d: A(LISTS[d][2], 0, 128)
+
+        def key_start(d):
+            kind, bits, bank = LISTS[d]
+            slots = A("c16", 896, 1024) if d == "own" else A("cp16") if d == 0 else A("c16", 128 * d, 128 * d + 128)
+
+            def f():
+                cbs = A("cb", 128 * bits, 128 * bits + 128, rows=(0, 64))
+                op("P", lambda q: q.matmul(key(d)[0], A("one", 0, 128, rows=(0, 64))[0], cbs[0], True, False),
+                   [A("one"), cbs, cb_hi], [key(d)])
+                mm(key(d), slots, A("i16"), False, False, pre=("pc", from_partner) if d == 0 and t == 0 else None)
+                if kind == "S":
+                    mm(key(d), A("nw16"), A("wt16"), False, False)
+            return f
+
+        def key_sum(d):
+            kind, bits, bank = LISTS[d]
+            wts = A("rw", 8, 16) if kind == "S" else A("rw", 0, 8)
+            pre = ("po%d" % t, from_partner) if d == "own" else ("pe%d" % t, 2 * from_partner) if d == 0 else None
+
+            def f():
+                for b in range(16):
+                    mm(A(bank, b, 128, 16), A(mbuf[d], b, V, 16), wts, False, b == 15, pre=pre if b == 0 else None)
+            return f
+
+        def merge(d, out, in0, needs=()):
+            return (MERGE, ["key%s" % d] + list(needs), lambda: tt(out, in0, key(d), ALU.min), "mg%s" % d)
+
+        def first(d, out):
+            return (MERGE, ["key%s" % d], lambda: act(out, key(d), ACT.Copy), "mg%s" % d)
+
+        def clear(buf, name):
+            return (MERGE, [], lambda: ts(buf, buf, -6145, None, ALU.bitwise_and), name)
+
+        def vgather(d, lo, hi, needs=()):
+            return (GV * (hi - lo) / V, [part(hi - 1)] + list(needs),
+                    lambda: gtt(A(mbuf[d], lo, hi), z, offs(d, lo, hi), A("w", lo, hi), ALU.min), "m%d_%d" % (d, hi))
+
+        gq.append((0.5, ["w2"], lambda: send(partner, A(mbuf["own"]), [z, A("w")], "po%d" % t), "own_in", 5.5))
+        for k in range(2):
+            lo = 1024 * k
+            sq.append((GS, [], (lambda lo=lo: gather("S", A(ze, lo, lo + 1024), z, offs(0, lo, lo + 1024))), "eg%d" % k))
+            gq.append((0.5, ["eg%d" % k], (lambda lo=lo: send(partner, A(mbuf[0], lo, lo + 1024), [A(ze, lo, lo + 1024), A("w", lo, lo + 1024)],
+                                                              "pe%d" % t)), "e_in%d" % k, 6.0))
+        gq.append((0.5, ["rclear"], lambda: send(partner, rin, [rk], "pr%d" % t), "r_in", 2.5))
+        ready = {"own": ["own_in"], 0: ["e_in0", "e_in1"], 3: [], 5: []}
+        pend = []
+        for k in range(4):
+            d, lo, zc = (3, 5)[k // 2], 1024 * (k % 2), 1024 * (k % 3)
+            sq.append((GS, ["cb"], (lambda d=d, lo=lo, zc=zc: gather("S", A("zc", zc, zc + 1024), z, offs(d, lo, lo + 1024))), "sg%d" % k))
+            sq.extend(pend)
+            if k == 1:
+                sq.append(first(1, A("bf")))
+            if k == 2:
+                sq.append(first("own", A("rf")))
+            pend = []
+            for j in range(2):
+                n = 2 * k + j
+                bank, c0, src = A("d%d" % (n % 3)), lo + 512 * j, A("zc", zc + 512 * j, zc + 512 * j + 512)
+
+                def diff(bank=bank, c0=c0, src=src):
+                    mm(bank, eye, A("w", c0, c0 + 512), True, False)
+                    mm(bank, neye, src, False, True)
+                pq.append((0.55, ["sg%d" % k, part(c0)] + (["sr%d" % (n - 3)] if n >= 3 else []), diff, "sd%d" % n))
+                pend.append((RELU, ["sd%d" % n], (lambda d=d, c0=c0, bank=bank: act(A(mbuf[d], c0, c0 + 512), bank, ACT.Relu)), "sr%d" % n))
+                ready[d].append("sr%d" % n)
+        sq.extend(pend)
+        bk = A("bk")
+        tail = (5, 6) if t == 0 else (6, 5)
+        if t == 0:
+            def wsum():
+                for b in range(16):
+                    mm(A("k0", b, 128, 16), A("w", b, V, 16), A("rw", 8, 16), True, True)
+            pq.append((0.55, ["w2"], wsum, "wsum"))
+            vq.extend([vgather(1, 0, 512), vgather(1, 512, 1024),
+                       (0.75, ["cin"], lambda: copy(A("cu", 256, 896), A("ci", 256, 896)), "cb"),
+                       (0.75, [], lambda: copy(A("c16", 256, 896), A("ci", 256, 896)), "cb16"),
+                       vgather(1, 1024, V),
+                       (0.2, ["wsum"], lambda: ts(A("wt16"), A("k0", 0, 128), 1.0 / 8192, -2048.0, ALU.mult, ALU.add), "wt")])
+        else:
+            vq.append(vgather(1, 0, V))
+        vq.extend([vgather(2, 0, V), vgather(4, 0, V, ["key1"]), merge(2, bk, A("bf"), ["mg1"]),
+                   vgather(6, 0, 1024),
+                   merge(0, rk, A("rf"), ["mgown"]), clear(rk, "rclear"),
+                   merge(3, bk, bk), merge(4, bk, bk), clear(bk, "clear"),
+                   (MERGE, [], lambda: ts(bk, bk, 2048.0, None, ALU.add), "lower"),
+                   vgather(6, 1024, V),
+                   (MERGE, ["r_in"], lambda: tt(bk, bk, rin, ALU.min, pre=("pr%d" % t, from_partner)), "mgr"),
+                   merge(tail[0], bk, bk), merge(tail[1], bk, bk)])
+        after = {0: ["key4"], "own": ["key2"], tail[1]: ["key%d" % tail[0]]}
+        bank_free = {}
+        for d in LISTS:
+            kind, bits, bank = LISTS[d]
+            if kind == "V":
+                ready[d] = ["m%d_%d" % (d, V)]
+            pq.append((0.2, bank_free.get(bank, []) + ["wt"] + (["cb16"] if d in (2, 3, 4, 5, 6) else []), key_start(d), "ks%s" % d))
+            pq.append((0.55, ["ks%s" % d] + ready[d] + after.get(d, []), key_sum(d), "key%s" % d))
+            bank_free[bank] = ["mg%s" % d]
+        for emit in arrange({"V": vq, "S": sq, "G": gq}, pq, known):
+            emit()
+
+    def trade_and_hand_on(t, zname, zn):
+        z = A(zname, 0, V)
+        split(A("bk"), 0)
+        mm(A("k3", 0, 256), A("hlb", 0, 128), A("ids", 0, 256), True, False)
+        mm(A("k3", 0, 256), A("hlb", 128, 256), A("ids", 128, 384), False, True)
+        copy(A("off"), A("k3", 0, 256))
+        banks = ["d0", "d1", "d2", "k4"]
+        for j in range(4):
+            for b in range(4 * j, 4 * j + 4):
+                mm(A(banks[j], 128 * (b % 4), 128 * (b % 4) + 128), (T.xw[:, :, :, b], "xw", 0, 16), eye, True, True)
+            if j % 2 == 0:
+                act(A("win", 512 * j, 512 * j + 512), A(banks[j]), ACT.Copy)
+            else:
+                copy(A("win", 512 * j, 512 * j + 512), A(banks[j]))
+        gather("S", A("f1", 1024, V), A("win"), A("off", 192, 256))
+        gather("V", A("f1", 0, 1024), A("win"), A("off", 128, 192))
+        gather("S", A("f2", 1024, V), A("f1"), A("off", 64, 128))
+        gather("V", A("f2", 0, 1024), A("f1"), A("off", 0, 64))
+        for b in range(16):
+            mm(A("k0", b, 256, 16), A("f2", b, V, 16), A("sel"), True, True)
+        gather("S", A(zname, V, V + 128), z, A("off", 0, 8))
+        tt(A("dd"), A("k3", 0, 128), A("at"), ALU.subtract)
+        tt(A("eq"), A("k0", 0, 256), A("aturn"), ALU.is_equal)
+        mm(A("k1", 0, NB), A("eq", 0, 128), A("ids", 384, 384 + NB), True, False)
+        mm(A("k1", 0, NB), A("eq", 128, 256), A("ids", 384, 384 + NB), False, True)
+        tt(A("u"), A("k1", 0, NB), A("thr"), ALU.is_lt)
+        op("V", lambda q: q.tensor_tensor_scan(A("s")[0], A("u")[0], A("u")[0], 0.0, ALU.add, ALU.max), [A("u")], [A("s")])
+        mm(A("k2", 0, NB), A("bo"), A("s"), True, True)
+        mm(A("d0", 0, NB), A("bo"), A("s"), True, True)
+        mm(A("d0", NB, 2 * NB), A("bo"), A("s"), True, False)
+        mm(A("d0", NB, 2 * NB), A("up"), A("u"), False, True)
+        tt(A("tm"), A("u", 0, 128), A("dd"), ALU.mult)
+        for h in range(6):
+            jk, kc, cn = A("junk", NB * h, NB * h + NB), A("kcol", h, h + 1), A("cnt", h, h + 1)
+            op("S", lambda q, jk=jk, kc=kc, cn=cn: q.activation(jk[0], A("k2", 0, NB)[0], ACT.Sign, bias=kc[0], scale=-1.0, accum_out=cn[0]),
+               [A("k2", 0, NB), kc], [jk, cn])
+        for h in (6, 7):
+            ts(A("le", 144 * (h - 6), 144 * (h - 6) + NB), A("d0", 0, NB), A("kcol", h, h + 1), 2.0, ALU.is_lt, ALU.mult)
+        copy(A("pp"), A("d0", NB, 2 * NB))
+        for h in (6, 7):
+            le, cn = A("le", 144 * (h - 6), 144 * (h - 6) + NB + 1), A("cnt", h, h + 1)
+            op("V", lambda q, le=le, cn=cn: q.tensor_reduce(cn[0], le[0], AxisListType.X, ALU.add), [le], [cn])
+        ts(A("offc"), A("cnt"), 0.5, NB / 2, ALU.mult, ALU.add)
+        gtt(A("oh"), A("pp"), A("offc"), A("krow"), ALU.is_equal)
+        ts(A("cbf"), A("cnt"), 0.5, NB / 2, ALU.mult, ALU.add)
+        for j in range(16):
+            mm(A("d1", 0, 8), A("zj", 15 - j, 143 - j), A("oh", j, 128, 16), j == 0, False)
+        mm(A("d1", 0, 8), A("ids", 0, 128), A("cbf"), False, True)
+        tt(A("tv"), A("k3", 0, 128), A("tm"), ALU.subtract)
+        copy(A("offg"), A("tv"))
+        gather("S", A(zn, TRADE_SPLIT, V), z, A("offg", TRADE_SPLIT // 16, 128))
+        copy(A("offt"), A("d1", 0, 8))
+        out, land = A("out%d" % t), A("land%d" % t)
+        gather("V", out, A(zname), A("offt"))
+        send(T.cores[(rank + 1 + t) % n_ranks], land, [out], "arr%d" % t)
+        n_in = len(topo.engines(T.cores[(rank - 1 - t) % n_ranks], core))
+        gather("V", A(zn, 0, TRADE_SPLIT), z, A("offg", 0, TRADE_SPLIT // 16))
+        copy(A("oi", 0, 8), A("offt"))
+        ts(A("oi", 8, 16), A("oi", 0, 8), V - 1, None, ALU.bitwise_and)
+        copy(A("offo"), A("oi", 8, 16))
+        new = A(zn, 0, V)
+        op("V", lambda q: q.tensor_copy(ind(new, A("offo")), land[0]), [A("offo"), land], [new], pre=("arr%d" % t, n_in))
+
+    zs = ["z0", "z1"]
+    for t in range(ROUNDS):
+        pointers(t, zs[t % 2])
+        trade_and_hand_on(t, zs[t % 2], zs[(t + 1) % 2])
+    last = A(zs[ROUNDS % 2], 0, V)
+    op("Y", lambda q: q.dma_start(T.y[:], last[0]), [last], [], sem=("st", 16))
+
+    def meet(a, b):
+        return a[0] == b[0] and (a[1] < b[2] and b[1] < a[2])
+
+    name = lambda o: o["sem"][0] if o["sem"] else o["eng"]
+    know = {e: {} for e in queue}
+    for i, o in enumerate(ops):
+        e = o["eng"]
+        need = {}
+        banks = set(a[0] for a in o["r"] + o["w"] if a[0] in PSUM)
+        for j in range(i):
+            p = ops[j]
+            if p["eng"] == "P" and e == "P":
+                continue
+            hit = any(meet(a, b) for a in o["r"] + o["w"] for b in p["w"]) or any(meet(a, b) for a in o["w"] for b in p["r"])
+            if not hit and banks and p["eng"] != e:
+                hit = any(b[0] in banks for b in p["r"] + p["w"])
+            if hit:
+                need[name(p)] = j
+        o["waits"] = []
+        for key, j in sorted(need.items(), key=lambda kv: -kv[1]):
+            if know[e].get(key, -1) < j:
+                o["waits"].append(j)
+                ops[j]["inc"] = True
+                for k2, v2 in ops[j]["know"].items():
+                    know[e][k2] = max(know[e].get(k2, -1), v2)
+        o["know"] = dict(know[e])
+        o["know"][name(o)] = i
+    count = {e: 0 for e in queue}
+    for o in ops:
+        e = o["eng"]
+        q = queue[e]
+        for j in o["waits"]:
+            q.wait_ge(T.sem[ops[j]["tok"][0]], ops[j]["tok"][1])
+        if o["pre"]:
+            q.wait_ge(T.sem[o["pre"][0]], o["pre"][1])
+        ins = o["fn"](q)
+        if o["sem"]:
+            o["tok"] = o["sem"][:2]
+            if len(o["sem"]) == 2:
+                ins.then_inc(T.sem[o["sem"][0]], 16)
+        elif o.get("inc"):
+            count[e] += 1
+            ins.then_inc(T.sem["e" + e], 1)
+            o["tok"] = ("e" + e, count[e])
+    for loc, n in left:
+        g.wait_ge(T.sem[loc], n)
+    g.wait_ge(T.sem.st, 16)

@@ -3,37 +3,41 @@ from concourse.mybir import AluOpType as ALU, AxisListType, ActivationFunctionTy
 
 V = 2048
 NB = 136
+HV = 5
 ROUNDS = 2
-TRADE_SPLIT = 768
+TAIL = 1536
+TRADE_SPLIT = 512
 BF, F32, I32, U16, F16 = "bfloat16", "float32", "int32", "uint16", "float16"
 
 SCRATCH = {}
 for _dt, _bufs in (
-        (BF, "z0 2176 z1 2176 w 2048 mv0 2048 mv1 2048 ms0 2048 ms1 2048 zc 3072 ze0 2048 ze1 2048 eo0 2048 eo1 2048 "
-             "ee0 2048 ee1 2048 win 2048 f1 2048 f2 2048 hlb 256 one 144 ids 640 i4k 128 bo 128 up 128 rw 16 sel 16 "
-             "zj 144 cb 512 eq 256 u 136 s 136 junk 1088 le 288 oh 128 cbf 8 out0 128 out1 128 land0 128 land1 128"),
-        (F16, "c16 1024 cp16 128 i16 128 nw16 128 wt16 128"),
-        (F32, "rcol 8 a16 128 at 128 thr 136 kcol 8 krow 128 bf 128 rf 128 dd 128 cnt 8 pp 136 tm 128 tv 128"),
-        (I32, "ci 896 hl 256 aturn 256 pcol 8 bk 128 rk0 128 rk1 128 rin0 128 rin1 128 oi 16"),
+        (BF, "z0 2176 z1 2176 w 2048 mv0 2048 mv1 2048 ms1 2048 zc 3072 ze0 2048 ze1 2048 eo0 2048 eo1 2048 "
+             "ee0 2048 ee1 2048 hlb 256 win 2048 f1 2048 f2 2048 one 144 eye 128 neye 128 i16x 128 i128x 128 bo 128 nbo 128 "
+             "st 128 nst 128 rw 16 zz 288 cb 256 zo 144 jj 688 ex 128 u 128 cum 144 junk 1088 le 688 sc 688 kb 8 pp 144 "
+             "oh 128 cbf 8 out0 128 out1 128 land0 128 land1 128"),
+        (F16, "c16 896 cp16 128 a16 128 i16 128 ni16 128 nw16 128 wt16 128 zx 128 tm 128"),
+        (F32, "aturn 128 at 128 kc 8 bf 128 rf 128 cnt 8"),
+        (I32, "ci 896 hl 256 bk 128 rk0 128 rk1 128 rin0 128 rin1 128 oi 16"),
         (U16, "cu 896 off 256 offc 8 offt 8 offo 8 offg 128")):
     _w = _bufs.split()
     for _k in range(0, len(_w), 2):
         SCRATCH[_w[_k]] = ("sbuf", [128, int(_w[_k + 1])], _dt)
 SCRATCH["xw"] = ("sbuf", [128, 8, 16, 16], BF)
-PSUM = ["d0", "d1", "d2", "k0", "k1", "k2", "k3", "k4"]
+PSUM = ["d0", "d1", "k0", "k1", "k2", "k3", "b0", "b1"]
 for _k in PSUM:
-    SCRATCH[_k] = ("psum", [128, 512], F32)
+    SCRATCH[_k] = ("psum", [128, 1024], BF) if _k[0] == "b" else ("psum", [128, 512], F32)
 
 LEFT = ["l%d" % _k for _k in range(11)]
-SEMAPHORES = ["eV", "eS", "eP", "eG", "ldca", "ldcb", "ldz", "ldw0", "ldw1", "ldw2", "st", "arr0", "arr1", "pc",
-              "po0", "po1", "pe0", "pe1", "pr0", "pr1"] + LEFT
+SEMAPHORES = ["eV", "eS", "eP", "eG", "ldc", "ldz", "ldw0", "ldw1", "ldw2", "st", "arr0", "arr1",
+              "pc", "po0", "po1", "pe0", "pe1", "pr0", "pr1"] + LEFT
 
-LISTS = {1: ("V", 0, "k0"), 2: ("V", 1, "k1"), "own": ("E", 0, "k2"), 0: ("E", 1, "k3"), 3: ("S", 2, "k4"),
-         4: ("V", 3, "k0"), 5: ("S", 2, "k1"), 6: ("V", 3, "k2")}
+LISTS = {6: ("V", 3, "k0"), 5: ("V", 2, "k1"), "own": ("E", -3, "k2"), 0: ("E", -1, "k3"), 4: ("V", 1, "k0"),
+         3: ("S", 0, "k1"), 1: ("V", -2, "k2"), 2: ("S", -1, "k3")}
+WINDOW = (("d0", "S", 3), ("b0", "V", 4), ("b1", "V", 4), ("d1", "S", 2), ("b0", "V", 3))
 
 
 def arrange(fixed, free, known):
-    done = dict(known)
+    done, near = dict(known), {}
     clock = {e: 0.0 for e in list(fixed) + ["P"]}
     pos = {e: 0 for e in fixed}
     free = list(free)
@@ -47,15 +51,16 @@ def arrange(fixed, free, known):
                     cands.append((max([clock[e]] + [done[n] for n in t[1]]), 1, e, t))
         for i, t in enumerate(free):
             if all(n in done for n in t[1]):
-                cands.append((max([clock["P"]] + [done[n] for n in t[1]]), 0, i, t))
+                cands.append((max([clock["P"]] + [near.get(n, done[n]) for n in t[1]]), 0, i, t))
         start, kind, who, t = min(cands, key=lambda c: (c[0], c[1], str(c[2]).rjust(4)))
         e = who if kind else "P"
         if kind:
             pos[e] += 1
         else:
             free.pop(who)
+            near[t[3]] = start + t[0]
         clock[e] = start + t[0]
-        done[t[3]] = clock[e] + (t[4] if len(t) > 4 else 0.05)
+        done[t[3]] = clock[e] + (t[4] if len(t) > 4 else 0.1)
         out.append(t[2])
     return out
 
@@ -70,13 +75,15 @@ def rank_program(g, core, T, topo):
     partner = by_die[place + 1 if place % 2 == 0 else place - 1]
     queue = {"V": g.vector, "S": g.scalar, "P": g.tensor, "G": g, "Y": g.sync}
     ops, left = [], []
-    pool = (None, "pool", 0, 1)
 
     def A(name, lo=0, hi=None, step=1, rows=None):
         hi = SCRATCH[name][1][1] if hi is None else hi
         r = slice(0, 128) if rows is None else slice(rows[0], rows[1])
         ap = T[name][r, lo:hi:step] if step > 1 else T[name][r, lo:hi]
         return (ap, name, lo, hi)
+
+    def X(ap, lo=0, hi=16):
+        return (ap, "xw", lo, hi)
 
     def op(eng, fn, reads, writes, sem=None, pre=None):
         ops.append({"eng": eng, "fn": fn, "r": [a[1:] for a in reads], "w": [a[1:] for a in writes], "sem": sem, "pre": pre})
@@ -101,6 +108,9 @@ def rank_program(g, core, T, topo):
         else:
             op("V", lambda q: q.tensor_scalar(out[0], a[0], v1, s2, op0, op1), rd, [out])
 
+    def scan(out, d0, d1, op0, op1):
+        op("V", lambda q: q.tensor_tensor_scan(out[0], d0[0], d1[0], 0.0, op0, op1), [d0, d1], [out])
+
     def gtt(out, win, off, b, alu):
         op("V", lambda q: q.tensor_tensor(out[0], ind(win, off), b[0], alu), [win, off, b], [out])
 
@@ -110,23 +120,17 @@ def rank_program(g, core, T, topo):
         else:
             op("S", lambda q: q.activation(out[0], ind(win, off), ACT.Copy), [win, off], [out])
 
-    def act(out, in_, func, scale=1.0, bias=None):
-        if bias is None:
-            op("S", lambda q: q.activation(out[0], in_[0], func, scale=scale), [in_], [out])
-        else:
-            op("S", lambda q: q.activation(out[0], in_[0], func, bias=bias[0], scale=scale), [in_, bias], [out])
+    def act(out, in_, func, scale=1.0):
+        op("S", lambda q: q.activation(out[0], in_[0], func, scale=scale), [in_], [out])
 
     def memset(out, val):
         op("V", lambda q: q.memset(out[0], val), [], [out])
 
-    def iota(out, pattern, base, mult, whole=False):
-        if whole:
-            op("G", lambda q: q.iota(out[0], pattern, base, mult), [], [out, pool])
-        else:
-            op("G", lambda q: q.iota(out[0], pattern, base, mult, allow_small_or_imprecise_dtypes=True), [], [out, pool])
+    def iota(out, pattern, base, mult):
+        op("G", lambda q: q.iota(out[0], pattern, base, mult, allow_small_or_imprecise_dtypes=True), [], [out])
 
     def select(out, in_, pattern, cmp, base, mult):
-        op("G", lambda q: q.affine_select(out[0], in_[0], pattern, cmp, 0.0, base, mult), [in_], [out, pool])
+        op("G", lambda q: q.affine_select(out[0], in_[0], pattern, cmp, 0.0, base, mult), [in_], [out])
 
     def load(eng, out, src, sem):
         op(eng, lambda q: q.dma_start(out[0], src), [], [out], sem=(sem, 16))
@@ -144,238 +148,264 @@ def rank_program(g, core, T, topo):
                                    srcs=[s[0] for s in srcs], dsts=[land[0]], alu_op=3)], local_sem=T.sem[loc])
         op("G", fn, srcs, [], sem=left[-1] + ("remote",))
 
-    def xrow(q):
-        return (T.xw[:, :, q, :], "xw", q, q + 1)
+    def lists_in(lo, hi):
+        copy(A("cu", 128 * lo, 128 * hi), A("ci", 128 * lo, 128 * hi))
 
-    def split(src, first):
-        ts(A("hl", 0, 128), src, 4, 127, ALU.arith_shift_right, ALU.bitwise_and)
-        ts(A("hl", 128, 256), src, 15, None, ALU.bitwise_and)
-        copy(A("hlb"), A("hl"))
-        act(xrow(first + 1), A("hlb", 128, 256), ACT.Copy)
-        copy(xrow(first), A("hlb", 0, 128))
+    def lists_half(lo, hi):
+        copy(A("c16", 128 * lo, 128 * hi), A("cu", 128 * lo, 128 * hi))
 
-    eye, neye = A("ids", 128, 256), A("ids", 512, 640)
+    eye, neye, bo, one = A("eye"), A("neye"), A("bo"), A("one", 0, 128)
     from_partner = len(topo.engines(partner, core))
 
-    load("S", A("ci", 0, 256), T.cand[:, 0:256], "ldca")
+    load("Y", A("ci"), T.cand[:], "ldc")
     load("Y", A("z0", 0, V), T.goods[:], "ldz")
     load("Y", A("w", 0, 512), T.wish[:, 0:512], "ldw0")
     load("Y", A("w", 512, 1024), T.wish[:, 512:1024], "ldw1")
-    load("Y", A("ci", 256, 896), T.cand[:, 256:896], "ldcb")
     load("Y", A("w", 1024, V), T.wish[:, 1024:V], "ldw2")
 
-    cb_hi = (T.cb[32:64, :], "cb_hi", 0, 512)
-    memset((T.xw[:], "xw", 0, 16), 0.0)
-    memset(cb_hi, float(1 << 19))
-    memset((T.cb[32:64, 256:384], "cb_hi", 256, 384), 0.0)
-    memset(A("le"), -float(NB))
-    iota(A("one"), [[0, 144]], 1, 0)
-    select(eye, A("one", 0, 128), [[-1, 128]], ALU.is_equal, 0, 1)
-    select(A("bo"), A("one", 0, 128), [[-16, 8], [0, 16]], ALU.is_ge, 0, 1)
-    select(A("bo"), A("bo"), [[16, 8], [0, 16]], ALU.is_ge, 15, -1)
-    iota(A("pcol", 0, 1), [[0, 1]], 0, 1, whole=True)
-    iota(A("a16"), [[16, 128]], 0, 0)
-    iota(A("aturn"), [[0, 16], [1, 16]], 0, 16, whole=True)
-    select(A("up"), A("bo"), [[-1, 128]], ALU.is_gt, 0, 1)
+    memset(A("one"), 1.0)
+    iota(A("aturn"), [[0, 8], [1, 16]], 0, 16)
+    select(eye, one, [[-1, 128]], ALU.is_equal, 0, 1)
+    select(bo, one, [[-16, 8], [0, 16]], ALU.is_ge, 0, 1)
+    select(bo, bo, [[16, 8], [0, 16]], ALU.is_ge, 15, -1)
+    select(A("st"), bo, [[-1, 128]], ALU.is_gt, 0, 1)
+    memset(A("cb", rows=(0, 8)), 2048.0)
+    memset(A("zz"), 0.0)
+    memset(A("cb", 0, 128, rows=(0, 2)), -14336.0)
+    memset(A("cb", 128, 256, rows=(0, 2)), -7168.0)
+    memset(A("zo", 0, 128), 0.0)
+    memset(A("cb", 0, 128, rows=(0, 1)), float(1 << 24))
+    memset(A("zo", 128, 144), 1.0)
+    copy(A("a16"), A("aturn"))
+    copy(A("i16"), eye)
+    ts(A("ni16"), eye, -1.0, None, ALU.mult)
+    ts(A("nw16"), eye, -8192.0, None, ALU.mult)
     act(neye, eye, ACT.Copy, -1.0)
-    act(A("ids", 0, 128), eye, ACT.Copy, 16.0)
-    act(A("ids", 256, 384), eye, ACT.Copy, 128.0)
-    act(A("ids", 384, 512), eye, ACT.Copy, 1.0)
-    act(A("i4k"), eye, ACT.Copy, 4096.0)
+    act(A("i16x"), eye, ACT.Copy, 16.0)
+    act(A("i128x"), eye, ACT.Copy, 128.0)
+    mm(A("k3", 0, 128), A("a16"), A("i16"), True, True)
+    act(A("at"), A("k3", 0, 128), ACT.Copy)
+    lists_in(0, 1)
+    tt(A("zz", 144 + 15, 144 + 128, 16), A("i16x", 0, 128, 16), A("eye", 1, 128, 16), ALU.add)
+    lists_half(0, 1)
+    send(partner, A("cp16"), [A("c16", 0, 128)], "pc")
     act(A("rw", 0, 8), A("bo", 0, 128, 16), ACT.Copy, -8192.0)
     act(A("rw", 8, 16), A("bo", 0, 128, 16), ACT.Copy, 8192.0)
-    ts(A("zj"), A("one"), 0.0, None, ALU.mult)
-    copy(A("i16"), eye)
-    ts(A("nw16"), eye, -8192.0, None, ALU.mult)
-    ts(A("pcol", 2, 3), A("pcol", 0, 1), 15, None, ALU.bitwise_and)
-    copy(A("rcol", 0, 1), A("pcol", 2, 3))
-    copy(A("cu", 0, 256), A("ci", 0, 256))
-    copy(A("c16", 0, 256), A("ci", 0, 256))
-    send(partner, A("cp16"), [A("c16", 0, 128)], "pc")
-    iota(A("cb", rows=(0, 32)), [[64, 4], [0, 128]], -256, 0)
-    iota(A("krow"), [[1, 128]], 4097, 0)
-    iota(A("thr", 0, 128), [[0, 128]], 1, 0)
-    iota(A("thr", 128, NB), [[0, 8]], 0, 0)
-    ts(A("zj", 15, 128, 16), A("bo", 0, 128, 16), A("rcol", 0, 1), None, ALU.mult)
-    tt(A("sel", 0, 8), A("ids", 0, 128, 16), A("ids", 129, 256, 16), ALU.add)
-    tt(A("sel", 8, 16), A("ids", 2, 128, 16), A("ids", 131, 256, 16), ALU.add)
-    act(A("at"), A("a16"), ACT.Identity, 1.0, A("rcol", 0, 1))
-    split(A("aturn", 0, 128), 2)
-    copy(A("c16", 896, 1024), A("at"))
-    ts(A("kcol"), A("at", 0, 8), 0.5, None, ALU.add)
-    tt(A("up"), A("i4k"), A("up"), ALU.subtract)
+    act(A("nbo"), bo, ACT.Copy, -1.0)
+    act(A("nst"), A("st"), ACT.Copy, -1.0)
+    copy(A("zz", 15, 128, 16), A("bo", 0, 128, 16))
+    copy(A("kb"), A("at", 0, 8))
+    ts(A("kc"), A("at", 0, 8), 0.5, None, ALU.add)
+    lists_in(1, 7)
+    lists_half(1, 7)
 
     def pointers(t, z):
-        GV, GS, RELU, MERGE = 3.4, 1.75, 0.6, 0.2
+        GV, GS, RELU, MERGE = 2.7, 1.38, 0.49, 0.11
         z = A(z, 0, V)
         vq, sq, pq, gq = [], [], [], []
         if t == 0:
-            known = {"w0": 0.5, "w1": 1.0, "cin": 2.3, "w2": 3.3}
+            known = {"w0": 0.5, "w1": 0.9, "w2": 1.8}
         else:
-            known = {"w0": 0.0, "w1": 0.0, "w2": 0.0, "cb": 0.0, "cb16": 0.0, "wt": 0.0}
+            known = {"w0": 0.0, "w1": 0.0, "w2": 0.0, "wt": 0.0}
         part = lambda col: "w%d" % min(col // 512, 2)
-        mbuf = {1: "mv0", 2: "mv1", 4: "mv0", 6: "mv1", 3: "ms0", 5: "ms1", "own": "eo%d" % t, 0: "ee%d" % t}
+        mbuf = {6: "mv0", 5: "mv1", 4: "mv0", 1: "mv1", 2: "ms1", "own": "eo%d" % t, 0: "ee%d" % t}
         ze, rk, rin = "ze%d" % t, A("rk%d" % t), A("rin%d" % t)
         offs = lambda d, lo, hi: A("cu", 128 * d + lo // 16, 128 * d + hi // 16)
         key = lambda d: A(LISTS[d][2], 0, 128)
 
         def key_start(d):
-            kind, bits, bank = LISTS[d]
-            slots = A("c16", 896, 1024) if d == "own" else A("cp16") if d == 0 else A("c16", 128 * d, 128 * d + 128)
+            kind, code, bank = LISTS[d]
+            block = 128 if kind == "S" else 0
 
             def f():
-                cbs = A("cb", 128 * bits, 128 * bits + 128, rows=(0, 64))
-                op("P", lambda q: q.matmul(key(d)[0], A("one", 0, 128, rows=(0, 64))[0], cbs[0], True, False),
-                   [A("one"), cbs, cb_hi], [key(d)])
-                mm(key(d), slots, A("i16"), False, False, pre=("pc", from_partner) if d == 0 and t == 0 else None)
+                mm(key(d), A("one", 0, 128, rows=(0, code + 5)), A("cb", block, block + 128, rows=(0, code + 5)), True, False)
+                if d == "own":
+                    mm(key(d), A("i16"), A("a16"), False, False)
+                else:
+                    slots = A("cp16") if d == 0 else A("c16", 128 * d, 128 * d + 128)
+                    mm(key(d), slots, A("i16"), False, False, pre=("pc", from_partner) if d == 0 and t == 0 else None)
                 if kind == "S":
                     mm(key(d), A("nw16"), A("wt16"), False, False)
             return f
 
-        def key_sum(d):
-            kind, bits, bank = LISTS[d]
+        def key_sum(d, lo, hi):
+            kind, code, bank = LISTS[d]
             wts = A("rw", 8, 16) if kind == "S" else A("rw", 0, 8)
             pre = ("po%d" % t, from_partner) if d == "own" else ("pe%d" % t, 2 * from_partner) if d == 0 else None
 
             def f():
                 for b in range(16):
-                    mm(A(bank, b, 128, 16), A(mbuf[d], b, V, 16), wts, False, b == 15, pre=pre if b == 0 else None)
+                    m = X(T.xw[:, :, :, b]) if d == 3 else A(mbuf[d], lo + b, hi, 16)
+                    mm(A(bank, b, 128, 16, rows=(lo // 16, hi // 16)), m, wts, False, b == 15, pre=pre if b == 0 else None)
             return f
 
         def merge(d, out, in0, needs=()):
             return (MERGE, ["key%s" % d] + list(needs), lambda: tt(out, in0, key(d), ALU.min), "mg%s" % d)
 
         def first(d, out):
-            return (MERGE, ["key%s" % d], lambda: act(out, key(d), ACT.Copy), "mg%s" % d)
+            return (0.17, ["key%s" % d], lambda: act(out, key(d), ACT.Copy), "mg%s" % d)
 
-        def clear(buf, name):
-            return (MERGE, [], lambda: ts(buf, buf, -6145, None, ALU.bitwise_and), name)
+        def clear(buf, bits, name):
+            return (MERGE, [], lambda: ts(buf, buf, -1 - bits, None, ALU.bitwise_and), name)
 
         def vgather(d, lo, hi, needs=()):
             return (GV * (hi - lo) / V, [part(hi - 1)] + list(needs),
                     lambda: gtt(A(mbuf[d], lo, hi), z, offs(d, lo, hi), A("w", lo, hi), ALU.min), "m%d_%d" % (d, hi))
 
-        gq.append((0.5, ["w2"], lambda: send(partner, A(mbuf["own"]), [z, A("w")], "po%d" % t), "own_in", 5.5))
+        own = (0.1, ["w2"], lambda: send(partner, A(mbuf["own"]), [z, A("w")], "po%d" % t), "own_in", 3.5)
         for k in range(2):
             lo = 1024 * k
             sq.append((GS, [], (lambda lo=lo: gather("S", A(ze, lo, lo + 1024), z, offs(0, lo, lo + 1024))), "eg%d" % k))
-            gq.append((0.5, ["eg%d" % k], (lambda lo=lo: send(partner, A(mbuf[0], lo, lo + 1024), [A(ze, lo, lo + 1024), A("w", lo, lo + 1024)],
-                                                              "pe%d" % t)), "e_in%d" % k, 6.0))
-        gq.append((0.5, ["rclear"], lambda: send(partner, rin, [rk], "pr%d" % t), "r_in", 2.5))
-        ready = {"own": ["own_in"], 0: ["e_in0", "e_in1"], 3: [], 5: []}
+            gq.append((0.1, ["eg%d" % k, "w%d" % (k + 1)],
+                       (lambda lo=lo: send(partner, A(mbuf[0], lo, lo + 1024), [A(ze, lo, lo + 1024), A("w", lo, lo + 1024)], "pe%d" % t)),
+                       "e_in%d" % k, 4.0))
+        gq.insert(1 - t, own)
+        if t == 0:
+            gq.append((1.3, [], lambda: iota(A("jj", 0, HV * NB), [[0, HV], [1, NB]], 0, 0), "jj"))
+        gq.append((0.1, ["rclear"], lambda: send(partner, rin, [rk], "pr%d" % t), "r_in", 1.5))
+        clipped = {3: [], 2: []}
         pend = []
         for k in range(4):
-            d, lo, zc = (3, 5)[k // 2], 1024 * (k % 2), 1024 * (k % 3)
-            sq.append((GS, ["cb"], (lambda d=d, lo=lo, zc=zc: gather("S", A("zc", zc, zc + 1024), z, offs(d, lo, lo + 1024))), "sg%d" % k))
+            d, lo, zc = (3, 2)[k // 2], 1024 * (k % 2), 1024 * (k % 3)
+            sq.append((GS, [],
+                       (lambda d=d, lo=lo, zc=zc: gather("S", A("zc", zc, zc + 1024), z, offs(d, lo, lo + 1024))), "sg%d" % k))
             sq.extend(pend)
             if k == 1:
-                sq.append(first(1, A("bf")))
+                sq.append(first(6, A("bf")))
             if k == 2:
                 sq.append(first("own", A("rf")))
             pend = []
             for j in range(2):
                 n = 2 * k + j
-                bank, c0, src = A("d%d" % (n % 3)), lo + 512 * j, A("zc", zc + 512 * j, zc + 512 * j + 512)
+                bank, c0, src = A("d%d" % (n % 2)), lo + 512 * j, A("zc", zc + 512 * j, zc + 512 * j + 512)
+                out = X(T.xw[:, c0 // 256:c0 // 256 + 2, :, :], c0 // 128, c0 // 128 + 4) if d == 3 else A(mbuf[d], c0, c0 + 512)
 
                 def diff(bank=bank, c0=c0, src=src):
                     mm(bank, eye, A("w", c0, c0 + 512), True, False)
                     mm(bank, neye, src, False, True)
-                pq.append((0.55, ["sg%d" % k, part(c0)] + (["sr%d" % (n - 3)] if n >= 3 else []), diff, "sd%d" % n))
-                pend.append((RELU, ["sd%d" % n], (lambda d=d, c0=c0, bank=bank: act(A(mbuf[d], c0, c0 + 512), bank, ACT.Relu)), "sr%d" % n))
-                ready[d].append("sr%d" % n)
+                pq.append((0.43, ["sg%d" % k, part(c0)] + (["sr%d" % (n - 2)] if n >= 2 else []), diff, "sd%d" % n))
+                pend.append((RELU, ["sd%d" % n], (lambda out=out, bank=bank: act(out, bank, ACT.Relu)), "sr%d" % n))
+                clipped[d].append("sr%d" % n)
         sq.extend(pend)
         bk = A("bk")
-        tail = (5, 6) if t == 0 else (6, 5)
+        tail = (2, 1) if t == 0 else (1, 2)
         if t == 0:
             def wsum():
                 for b in range(16):
-                    mm(A("k0", b, 128, 16), A("w", b, V, 16), A("rw", 8, 16), True, True)
-            pq.append((0.55, ["w2"], wsum, "wsum"))
-            vq.extend([vgather(1, 0, 512), vgather(1, 512, 1024),
-                       (0.75, ["cin"], lambda: copy(A("cu", 256, 896), A("ci", 256, 896)), "cb"),
-                       (0.75, [], lambda: copy(A("c16", 256, 896), A("ci", 256, 896)), "cb16"),
-                       vgather(1, 1024, V),
-                       (0.2, ["wsum"], lambda: ts(A("wt16"), A("k0", 0, 128), 1.0 / 8192, -2048.0, ALU.mult, ALU.add), "wt")])
+                    mm(A("k1", b, 128, 16), A("w", b, V, 16), A("rw", 8, 16), True, True)
+            pq.append((0.43, ["w2"], wsum, "wsum"))
+            vq.extend([vgather(6, 0, 512), vgather(6, 512, 1024), vgather(6, 1024, V),
+                       (0.11, ["wsum"], lambda: ts(A("wt16"), A("k1", 0, 128), 1.0 / 8192, -2048.0, ALU.mult, ALU.add), "wt"),
+                       vgather(5, 0, V)])
         else:
-            vq.append(vgather(1, 0, V))
-        vq.extend([vgather(2, 0, V), vgather(4, 0, V, ["key1"]), merge(2, bk, A("bf"), ["mg1"]),
-                   vgather(6, 0, 1024),
-                   merge(0, rk, A("rf"), ["mgown"]), clear(rk, "rclear"),
-                   merge(3, bk, bk), merge(4, bk, bk), clear(bk, "clear"),
-                   (MERGE, [], lambda: ts(bk, bk, 2048.0, None, ALU.add), "lower"),
-                   vgather(6, 1024, V),
-                   (MERGE, ["r_in"], lambda: tt(bk, bk, rin, ALU.min, pre=("pr%d" % t, from_partner)), "mgr"),
+            vq.extend([vgather(6, 0, V), vgather(5, 0, V)])
+        vq.extend([vgather(4, 0, 1024, ["key6"]), merge(5, bk, A("bf"), ["mg6"]), vgather(4, 1024, V),
+                   vgather(1, 0, 768), merge(0, rk, A("rf"), ["mgown"]), merge(4, bk, bk), clear(rk, 4096, "rclear"),
+                   vgather(1, 768, TAIL), merge(3, bk, bk),
+                   vgather(1, TAIL, V), clear(bk, 6144, "clear"),
+                   (2 * MERGE, ["r_in"], lambda: tt(bk, bk, rin, ALU.min, pre=("pr%d" % t, from_partner)), "mgr"),
                    merge(tail[0], bk, bk), merge(tail[1], bk, bk)])
-        after = {0: ["key4"], "own": ["key2"], tail[1]: ["key%d" % tail[0]]}
+        ready = {"own": ["own_in", "key5"], 0: ["e_in0", "e_in1", "key4"], 3: clipped[3]}
         bank_free = {}
         for d in LISTS:
-            kind, bits, bank = LISTS[d]
-            if kind == "V":
-                ready[d] = ["m%d_%d" % (d, V)]
-            pq.append((0.2, bank_free.get(bank, []) + ["wt"] + (["cb16"] if d in (2, 3, 4, 5, 6) else []), key_start(d), "ks%s" % d))
-            pq.append((0.55, ["ks%s" % d] + ready[d] + after.get(d, []), key_sum(d), "key%s" % d))
+            kind, code, bank = LISTS[d]
+            pq.append((0.15, bank_free.get(bank, []) + ["wt"], key_start(d), "ks%s" % d))
+            if d in tail:
+                a, b = (["m1_%d" % TAIL], ["m1_%d" % V]) if d == 1 else (clipped[2][:3], clipped[2][3:])
+                pq.append((0.43, ["ks%s" % d] + a, key_sum(d, 0, TAIL), "part%s" % d))
+                pq.append((0.22, ["part%s" % d] + b + (["key%d" % tail[0]] if d == tail[1] else []), key_sum(d, TAIL, V), "key%s" % d))
+            else:
+                pq.append((0.43, ["ks%s" % d] + ready.get(d, ["m%s_%d" % (d, V)]), key_sum(d, 0, V), "key%s" % d))
             bank_free[bank] = ["mg%s" % d]
         for emit in arrange({"V": vq, "S": sq, "G": gq}, pq, known):
             emit()
 
     def trade_and_hand_on(t, zname, zn):
         z = A(zname, 0, V)
-        split(A("bk"), 0)
-        mm(A("k3", 0, 256), A("hlb", 0, 128), A("ids", 0, 256), True, False)
-        mm(A("k3", 0, 256), A("hlb", 128, 256), A("ids", 128, 384), False, True)
-        copy(A("off"), A("k3", 0, 256))
-        banks = ["d0", "d1", "d2", "k4"]
-        for j in range(4):
-            for b in range(4 * j, 4 * j + 4):
-                mm(A(banks[j], 128 * (b % 4), 128 * (b % 4) + 128), (T.xw[:, :, :, b], "xw", 0, 16), eye, True, True)
-            if j % 2 == 0:
-                act(A("win", 512 * j, 512 * j + 512), A(banks[j]), ACT.Copy)
+        hi, lo = A("hlb", 0, 128), A("hlb", 128, 256)
+
+        def plain(out, stop):
+            mm(out, hi, A("i16x"), True, False)
+            mm(out, lo, eye, False, stop)
+
+        def to_list(out, src, c0, c1, start):
+            for b in range(16):
+                mm(A(out, c0, c1), A("zz", 144 + 15 - b, 144 + 143 - b), A(src, 16 * c0 + b, 16 * c1, 16), start and b == 0, start and b == 15)
+        ts(A("hl", 0, 128), A("bk"), 4, 127, ALU.arith_shift_right, ALU.bitwise_and)
+        ts(A("hl", 128, 256), A("bk"), 15, None, ALU.bitwise_and)
+        copy(X(T.xw[:, :, 0, :], 0, 1), A("hl", 0, 128))
+        copy(X(T.xw[:, :, 1, :], 1, 2), A("hl", 128, 256))
+        copy(A("hlb"), A("hl"))
+        b = 0
+        for bank, eng, n in WINDOW:
+            if bank == "d1":
+                mm(A("k0", 128, 256), hi, eye, True, False)
+                mm(A("k0", 128, 256), lo, A("i128x"), False, True)
+                copy(A("off", 128, 256), A("k0", 128, 256))
+            for j in range(n):
+                src, dst = X(T.xw[:, :, :, b + j]), A(bank, 128 * j, 128 * j + 128)
+                if eng == "S":
+                    mm(dst, src, eye, True, True)
+                else:
+                    op("P", lambda q, src=src, dst=dst: q.transpose(dst[0], src[0], eye[0]), [src, eye], [dst])
+            if eng == "S":
+                act(A("win", 128 * b, 128 * (b + n)), A(bank, 0, 128 * n), ACT.Copy)
             else:
-                copy(A("win", 512 * j, 512 * j + 512), A(banks[j]))
-        gather("S", A("f1", 1024, V), A("win"), A("off", 192, 256))
-        gather("V", A("f1", 0, 1024), A("win"), A("off", 128, 192))
-        gather("S", A("f2", 1024, V), A("f1"), A("off", 64, 128))
-        gather("V", A("f2", 0, 1024), A("f1"), A("off", 0, 64))
-        for b in range(16):
-            mm(A("k0", b, 256, 16), A("f2", b, V, 16), A("sel"), True, True)
+                copy(A("win", 128 * b, 128 * (b + n)), A(bank, 0, 128 * n))
+            b += n
+        plain(A("k2", 0, 128), True)
+        dd = A("k1", 0, 128)
+        plain(dd, False)
+        mm(dd, A("a16"), A("ni16"), False, True)
+        gather("S", A("f1", 960, V), A("win"), A("off", 128 + 60, 256))
+        gather("V", A("f1", 0, 960), A("win"), A("off", 128, 128 + 60))
+        copy(A("off", 0, 128), A("k2", 0, 128))
+        mm(A("d0", 0, NB), bo, A("zo", 0, NB), True, False)
+        mm(A("d1", 0, NB), A("nst"), A("zo", 0, NB), True, False)
+        plain(A("k0", 0, 128), False)
+        for k in range(4):
+            gather("VS"[k % 2], A("f2", 512 * k, 512 * k + 512), A("f1"), A("off", 32 * k, 32 * k + 32))
+        to_list("k2", "f1", 0, 128, True)
+        mm(A("k3", 0, 128), eye, A("zo", 0, 128), True, False)
+        to_list("k3", "f2", 0, 64, False)
+        to_list("k3", "f2", 64, 128, False)
         gather("S", A(zname, V, V + 128), z, A("off", 0, 8))
-        tt(A("dd"), A("k3", 0, 128), A("at"), ALU.subtract)
-        tt(A("eq"), A("k0", 0, 256), A("aturn"), ALU.is_equal)
-        mm(A("k1", 0, NB), A("eq", 0, 128), A("ids", 384, 384 + NB), True, False)
-        mm(A("k1", 0, NB), A("eq", 128, 256), A("ids", 384, 384 + NB), False, True)
-        tt(A("u"), A("k1", 0, NB), A("thr"), ALU.is_lt)
-        op("V", lambda q: q.tensor_tensor_scan(A("s")[0], A("u")[0], A("u")[0], 0.0, ALU.add, ALU.max), [A("u")], [A("s")])
-        mm(A("k2", 0, NB), A("bo"), A("s"), True, True)
-        mm(A("d0", 0, NB), A("bo"), A("s"), True, True)
-        mm(A("d0", NB, 2 * NB), A("bo"), A("s"), True, False)
-        mm(A("d0", NB, 2 * NB), A("up"), A("u"), False, True)
-        tt(A("tm"), A("u", 0, 128), A("dd"), ALU.mult)
-        for h in range(6):
-            jk, kc, cn = A("junk", NB * h, NB * h + NB), A("kcol", h, h + 1), A("cnt", h, h + 1)
-            op("S", lambda q, jk=jk, kc=kc, cn=cn: q.activation(jk[0], A("k2", 0, NB)[0], ACT.Sign, bias=kc[0], scale=-1.0, accum_out=cn[0]),
-               [A("k2", 0, NB), kc], [jk, cn])
-        for h in (6, 7):
-            ts(A("le", 144 * (h - 6), 144 * (h - 6) + NB), A("d0", 0, NB), A("kcol", h, h + 1), 2.0, ALU.is_lt, ALU.mult)
-        copy(A("pp"), A("d0", NB, 2 * NB))
-        for h in (6, 7):
-            le, cn = A("le", 144 * (h - 6), 144 * (h - 6) + NB + 1), A("cnt", h, h + 1)
-            op("V", lambda q, le=le, cn=cn: q.tensor_reduce(cn[0], le[0], AxisListType.X, ALU.add), [le], [cn])
-        ts(A("offc"), A("cnt"), 0.5, NB / 2, ALU.mult, ALU.add)
-        gtt(A("oh"), A("pp"), A("offc"), A("krow"), ALU.is_equal)
-        ts(A("cbf"), A("cnt"), 0.5, NB / 2, ALU.mult, ALU.add)
+        tt(A("ex"), A("k2", 0, 128), A("at"), ALU.is_equal)
+        tt(A("zx"), A("ex"), dd, ALU.mult)
+        mm(A("k3", 0, 128), A("ni16"), A("zx"), False, True)
+        tt(A("u"), A("k3", 0, 128), A("at"), ALU.not_equal)
+        mm(A("d0", 0, 128), bo, A("u"), False, False)
+        mm(A("d0", 128, NB), A("nbo"), A("u", 0, 8), False, True)
+        mm(A("d1", 0, 128), A("nst"), A("u"), False, False)
+        mm(A("d1", 128, NB), A("st"), A("u", 0, 8), False, True)
+        tt(A("tm"), A("u"), dd, ALU.mult)
+        mm(A("k0", 0, 128), A("ni16"), A("tm"), False, True)
+        cum = A("cum", 0, NB)
+        scan(cum, A("d0", 0, NB), A("one", 0, NB), ALU.add, ALU.mult)
+        for h in range(HV, 8):
+            jk, kc, cn = A("junk", NB * h, NB * h + NB), A("kc", h, h + 1), A("cnt", h, h + 1)
+            op("S", lambda q, jk=jk, kc=kc, cn=cn: q.activation(jk[0], cum[0], ACT.Sign, bias=kc[0], scale=-1.0, accum_out=cn[0]),
+               [cum, kc], [jk, cn])
+        for h in range(HV):
+            ts(A("le", NB * h, NB * h + NB), cum, A("kb", h, h + 1), None, ALU.is_le)
+        tt(A("pp", 0, NB), A("d1", 0, NB), cum, ALU.add)
+        scan(A("sc", 0, HV * NB), A("jj", 0, HV * NB), A("le", 0, HV * NB), ALU.min, ALU.add)
+        ts(A("offc", HV, 8), A("cnt", HV, 8), 0.5, NB / 2, ALU.mult, ALU.add)
+        copy(A("offc", 0, HV), A("sc", NB - 1, HV * NB, NB))
+        gtt(A("oh"), A("pp", 0, NB), A("offc"), A("jj", 0, 128), ALU.is_le)
+        copy(A("cbf"), A("offc"))
+        copy(A("offg"), A("k0", 0, 128))
         for j in range(16):
-            mm(A("d1", 0, 8), A("zj", 15 - j, 143 - j), A("oh", j, 128, 16), j == 0, False)
-        mm(A("d1", 0, 8), A("ids", 0, 128), A("cbf"), False, True)
-        tt(A("tv"), A("k3", 0, 128), A("tm"), ALU.subtract)
-        copy(A("offg"), A("tv"))
+            mm(A("k2", 0, 8), A("zz", 15 - j, 143 - j), A("oh", j, 128, 16), j == 0, False)
+        mm(A("k2", 0, 8), A("i16x"), A("cbf"), False, True)
         gather("S", A(zn, TRADE_SPLIT, V), z, A("offg", TRADE_SPLIT // 16, 128))
-        copy(A("offt"), A("d1", 0, 8))
+        copy(A("offt"), A("k2", 0, 8))
         out, land = A("out%d" % t), A("land%d" % t)
         gather("V", out, A(zname), A("offt"))
         send(T.cores[(rank + 1 + t) % n_ranks], land, [out], "arr%d" % t)
         n_in = len(topo.engines(T.cores[(rank - 1 - t) % n_ranks], core))
-        gather("V", A(zn, 0, TRADE_SPLIT), z, A("offg", 0, TRADE_SPLIT // 16))
         copy(A("oi", 0, 8), A("offt"))
+        gather("V", A(zn, 0, TRADE_SPLIT), z, A("offg", 0, TRADE_SPLIT // 16))
         ts(A("oi", 8, 16), A("oi", 0, 8), V - 1, None, ALU.bitwise_and)
         copy(A("offo"), A("oi", 8, 16))
         new = A(zn, 0, V)

@@ -1,21 +1,20 @@
 from concourse.bass import DstId, RemoteDMATransfer
-from concourse.mybir import AluOpType as ALU, AxisListType, ActivationFunctionType as ACT
+from concourse.mybir import AluOpType as ALU, ActivationFunctionType as ACT
 
 V = 2048
 NB = 136
 HV = 5
 ROUNDS = 2
-TAIL = 1536
-TRADE_SPLIT = 512
+TRADE_SPLIT = 384
 BF, F32, I32, U16, F16 = "bfloat16", "float32", "int32", "uint16", "float16"
 
 SCRATCH = {}
 for _dt, _bufs in (
-        (BF, "z0 2176 z1 2176 w 2048 mv0 2048 mv1 2048 ms1 2048 zc 3072 ze0 2048 ze1 2048 eo0 2048 eo1 2048 "
-             "ee0 2048 ee1 2048 hlb 256 win 2048 f1 2048 f2 2048 one 144 eye 128 neye 128 i16x 128 i128x 128 bo 128 nbo 128 "
-             "st 128 nst 128 rw 16 zz 288 cb 256 zo 144 jj 688 ex 128 u 128 cum 144 junk 1088 le 688 sc 688 kb 8 pp 144 "
-             "oh 128 cbf 8 out0 128 out1 128 land0 128 land1 128"),
-        (F16, "c16 896 cp16 128 a16 128 i16 128 ni16 128 nw16 128 wt16 128 zx 128 tm 128"),
+        (BF, "z0 2176 z1 2176 w 2048 mv0 2048 mv1 2048 ms 2048 zc2 2048 zc3 2048 ze0 2048 ze1 2048 eo0 2048 eo1 2048 ex1 2048 "
+             "ee0 2048 ee1 2048 hlb 256 win 2048 f1 2048 f2 2048 one 144 eye 128 neye 128 nw 128 i16x 128 i128x 128 "
+             "bo 128 nbo 128 st 128 nst 128 rw 16 zz 288 cb 1024 zo 144 jj 688 ex 128 u 128 cum 144 junk 1088 le 688 "
+             "sc 688 kb 8 pp 144 oh 128 cbf 8 out0 128 out1 128 land0 128 land1 128"),
+        (F16, "c16 896 cp16 384 a16 128 wt16 128 zx 128 tm 128"),
         (F32, "aturn 128 at 128 kc 8 bf 128 rf 128 cnt 8"),
         (I32, "ci 896 hl 256 bk 128 rk0 128 rk1 128 rin0 128 rin1 128 oi 16"),
         (U16, "cu 896 off 256 offc 8 offt 8 offo 8 offg 128")):
@@ -27,41 +26,38 @@ PSUM = ["d0", "d1", "k0", "k1", "k2", "k3", "b0", "b1"]
 for _k in PSUM:
     SCRATCH[_k] = ("psum", [128, 1024], BF) if _k[0] == "b" else ("psum", [128, 512], F32)
 
-LEFT = ["l%d" % _k for _k in range(11)]
+LEFT = ["l%d" % _k for _k in range(12)]
 SEMAPHORES = ["eV", "eS", "eP", "eG", "ldc", "ldz", "ldw0", "ldw1", "ldw2", "st", "arr0", "arr1",
-              "pc", "po0", "po1", "pe0", "pe1", "pr0", "pr1"] + LEFT
+              "pc", "po0", "po1", "pe0", "pe1", "px1", "py", "pr0", "pr1"] + LEFT
 
-LISTS = {6: ("V", 3, "k0"), 5: ("V", 2, "k1"), "own": ("E", -3, "k2"), 0: ("E", -1, "k3"), 4: ("V", 1, "k0"),
-         3: ("S", 0, "k1"), 1: ("V", -2, "k2"), 2: ("S", -1, "k3")}
+LISTS = {"6": (3, "k0", 0), "o": (-3, "k0", 128), "4": (1, "k0", 256), "1": (-2, "k0", 384),
+         "5": (2, "k1", 0), "0": (-1, "k1", 128), "2": (-1, "k1", 256), "3": (0, "k1", 384), "x": (-1, "k0", 0)}
+ORDER = [
+    {"V": "g0.7.8 g6.0.2 g6.2.5 g6.5.8 t g5.0.8 g4.0.4 m5 g4.4.8 g1.0.4 m4 m0 m3 ar g1.4.6 ab g1.6.8 mE m2 m1",
+     "S": "g0.0.4 g0.4.7 g3.0.4 g3.4.8 r3.0 r3.1 m6 g2.0.4 r3.2 r3.3 g2.4.8 mo r2.0 r2.1 r2.2 r2.3 c",
+     "P": "k6 k5 w3.0.d0 w3.1.d1 ws w3.2.k2 z3.0 z3.1 p6.0.4 ko w3.3.k3 z3.2 z3.3 w2.0.d0 w2.1.d1 p5.0.4 k3 z2.0 z2.1 "
+          "po.0.4 k4 p3.0.4 k0 p4.0.4 p0.0.4 w2.2.k2 w2.3.k3 z2.2 z2.3 k1 k2 p1.0.3 p2.0.4 p1.3.4",
+     "G": "f0.0.4 fo f0.4.8 j s y"},
+    {"V": "g6.0.8 g5.0.8 g4.0.4 m5 g4.4.8 g1.0.4 m0 m4 ar mx g1.4.6 m3 g1.6.7 ab g1.7.8 mE m2 m1",
+     "S": "g0.0.8 g2.4.8 m6 g3.0.4 g3.4.8 r3.0 r3.1 mo g2.0.2 r3.2 r3.3 g2.2.4 r2.0 r2.1",
+     "P": "k6 k5 w3.0.d0 w3.1.d1 w3.2.k2 w3.3.k3 p6.0.4 ko p5.0.4 k0 z3.0 z3.1 po.0.4 k4 z3.2 z3.3 p0.0.4 k3 p4.0.4 "
+          "kx w2.0.d0 px.2.4 z2.0 w2.1.d1 p3.0.4<m0 k1<mx z2.1 p1.0.3 k2 p2.0.1 p2.1.2 p1.3.4",
+     "G": "fo f0.0.8 fx.4.8 s"}]
+WISH = (0, 512, 1280, V)
+LANDED = {"w0": 0.5, "w1": 0.9, "w2": 1.8}
 WINDOW = (("d0", "S", 3), ("b0", "V", 4), ("b1", "V", 4), ("d1", "S", 2), ("b0", "V", 3))
 
 
-def arrange(fixed, free, known):
-    done, near = dict(known), {}
-    clock = {e: 0.0 for e in list(fixed) + ["P"]}
-    pos = {e: 0 for e in fixed}
-    free = list(free)
-    out = []
-    while free or any(pos[e] < len(fixed[e]) for e in fixed):
-        cands = []
-        for e in fixed:
-            if pos[e] < len(fixed[e]):
-                t = fixed[e][pos[e]]
-                if all(n in done for n in t[1]):
-                    cands.append((max([clock[e]] + [done[n] for n in t[1]]), 1, e, t))
-        for i, t in enumerate(free):
-            if all(n in done for n in t[1]):
-                cands.append((max([clock["P"]] + [near.get(n, done[n]) for n in t[1]]), 0, i, t))
-        start, kind, who, t = min(cands, key=lambda c: (c[0], c[1], str(c[2]).rjust(4)))
-        e = who if kind else "P"
-        if kind:
-            pos[e] += 1
-        else:
-            free.pop(who)
-            near[t[3]] = start + t[0]
-        clock[e] = start + t[0]
-        done[t[3]] = clock[e] + (t[4] if len(t) > 4 else 0.1)
-        out.append(t[2])
+def arrange(queues, known):
+    done, clock, pos, out = dict(known), dict.fromkeys(queues, 0.0), dict.fromkeys(queues, 0), []
+    while any(pos[e] < len(queues[e]) for e in queues):
+        heads = [(e, queues[e][pos[e]]) for e in queues if pos[e] < len(queues[e])]
+        start, e, t = min([(max([clock[e]] + [done[n] for n in t[2]]), e, t) for e, t in heads if all(n in done for n in t[2])],
+                          key=lambda c: c[:2])
+        pos[e] += 1
+        clock[e] = start + t[1]
+        done[t[0]] = clock[e] + (t[4] if len(t) > 4 else 0.1)
+        out.append(t[3])
     return out
 
 
@@ -159,165 +155,154 @@ def rank_program(g, core, T, topo):
 
     load("Y", A("ci"), T.cand[:], "ldc")
     load("Y", A("z0", 0, V), T.goods[:], "ldz")
-    load("Y", A("w", 0, 512), T.wish[:, 0:512], "ldw0")
-    load("Y", A("w", 512, 1024), T.wish[:, 512:1024], "ldw1")
-    load("Y", A("w", 1024, V), T.wish[:, 1024:V], "ldw2")
+    for k in range(3):
+        load("Y", A("w", WISH[k], WISH[k + 1]), T.wish[:, WISH[k]:WISH[k + 1]], "ldw%d" % k)
 
     memset(A("one"), 1.0)
-    iota(A("aturn"), [[0, 8], [1, 16]], 0, 16)
     select(eye, one, [[-1, 128]], ALU.is_equal, 0, 1)
+    iota(A("aturn"), [[0, 8], [1, 16]], 0, 16)
     select(bo, one, [[-16, 8], [0, 16]], ALU.is_ge, 0, 1)
     select(bo, bo, [[16, 8], [0, 16]], ALU.is_ge, 15, -1)
     select(A("st"), bo, [[-1, 128]], ALU.is_gt, 0, 1)
-    memset(A("cb", rows=(0, 8)), 2048.0)
+    for code, bank, col in [LISTS[d] for d in "o0123456"]:
+        at = 512 * int(bank[1]) + col
+        memset(A("cb", at, at + 128, rows=(0, 2)), 2048.0 * code - 8192.0)
     memset(A("zz"), 0.0)
-    memset(A("cb", 0, 128, rows=(0, 2)), -14336.0)
-    memset(A("cb", 128, 256, rows=(0, 2)), -7168.0)
+    memset(A("cb", 0, 768, rows=(0, 1)), float(1 << 24))
+    memset(A("cb", 768, 1024, rows=(0, 1)), 0.0)
     memset(A("zo", 0, 128), 0.0)
-    memset(A("cb", 0, 128, rows=(0, 1)), float(1 << 24))
     memset(A("zo", 128, 144), 1.0)
     copy(A("a16"), A("aturn"))
-    copy(A("i16"), eye)
-    ts(A("ni16"), eye, -1.0, None, ALU.mult)
-    ts(A("nw16"), eye, -8192.0, None, ALU.mult)
     act(neye, eye, ACT.Copy, -1.0)
-    act(A("i16x"), eye, ACT.Copy, 16.0)
-    act(A("i128x"), eye, ACT.Copy, 128.0)
-    mm(A("k3", 0, 128), A("a16"), A("i16"), True, True)
+    act(A("nw"), eye, ACT.Copy, -8192.0)
+    mm(A("k3", 0, 128), A("a16"), eye, True, True)
     act(A("at"), A("k3", 0, 128), ACT.Copy)
-    lists_in(0, 1)
-    tt(A("zz", 144 + 15, 144 + 128, 16), A("i16x", 0, 128, 16), A("eye", 1, 128, 16), ALU.add)
-    lists_half(0, 1)
-    send(partner, A("cp16"), [A("c16", 0, 128)], "pc")
     act(A("rw", 0, 8), A("bo", 0, 128, 16), ACT.Copy, -8192.0)
     act(A("rw", 8, 16), A("bo", 0, 128, 16), ACT.Copy, 8192.0)
-    act(A("nbo"), bo, ACT.Copy, -1.0)
-    act(A("nst"), A("st"), ACT.Copy, -1.0)
-    copy(A("zz", 15, 128, 16), A("bo", 0, 128, 16))
-    copy(A("kb"), A("at", 0, 8))
-    ts(A("kc"), A("at", 0, 8), 0.5, None, ALU.add)
+    lists_in(0, 1)
     lists_in(1, 7)
+    lists_half(0, 1)
+    send(partner, A("cp16", 0, 128), [A("c16", 0, 128)], "pc")
     lists_half(1, 7)
 
+    def later_constants():
+        act(A("i16x"), eye, ACT.Copy, 16.0)
+        act(A("i128x"), eye, ACT.Copy, 128.0)
+        act(A("nbo"), bo, ACT.Copy, -1.0)
+        act(A("nst"), A("st"), ACT.Copy, -1.0)
+        act(A("zz", 15, 128, 16), A("bo", 0, 128, 16), ACT.Copy)
+        act(A("kb"), A("at", 0, 8), ACT.Copy)
+        op("S", lambda q: q.activation(T.kc[:], T.at[:, 0:8], ACT.Identity, bias=0.5), [A("at")], [A("kc")])
+
     def pointers(t, z):
-        GV, GS, RELU, MERGE = 2.7, 1.38, 0.49, 0.11
         z = A(z, 0, V)
-        vq, sq, pq, gq = [], [], [], []
-        if t == 0:
-            known = {"w0": 0.5, "w1": 0.9, "w2": 1.8}
-        else:
-            known = {"w0": 0.0, "w1": 0.0, "w2": 0.0, "wt": 0.0}
-        part = lambda col: "w%d" % min(col // 512, 2)
-        mbuf = {6: "mv0", 5: "mv1", 4: "mv0", 1: "mv1", 2: "ms1", "own": "eo%d" % t, 0: "ee%d" % t}
-        ze, rk, rin = "ze%d" % t, A("rk%d" % t), A("rin%d" % t)
-        offs = lambda d, lo, hi: A("cu", 128 * d + lo // 16, 128 * d + hi // 16)
-        key = lambda d: A(LISTS[d][2], 0, 128)
+        after = {n.split("<")[0]: n.split("<")[1:] for e in "VSPG" for n in ORDER[t][e].split()}
+        order = {e: [n.split("<")[0] for n in ORDER[t][e].split()] for e in "VSPG"}
+        names = [n for e in order for n in order[e]]
+        args = lambda n: n[1:].split(".")
+        span = lambda n, unit: (unit * int(args(n)[1]), unit * int(args(n)[2]))
+        gathers = lambda d, lo, hi: [n for n in names if n[:2] == "g" + d and span(n, 256)[0] < hi and lo < span(n, 256)[1]]
+        clipped = lambda d, col: "r%s.%d" % (d, col // 512) in names
+        wish = lambda hi: "w%d" % ((hi > WISH[1]) + (hi > WISH[2]))
+        mbuf = {"6": "mv0", "5": "mv1", "4": "mv0", "1": "mv1", "2": "ms", "o": "eo%d" % t, "0": "ee%d" % t, "x": "ex%d" % t}
+        raw = {"0": "ze%d" % t, "3": "zc3", "2": "zc2", "x": "zc2"}
+        bk, rk, rin = A("bk"), A("rk%d" % t), A("rin%d" % t)
+        cut = min([span(n, 256)[0] // 16 for n in order["G"] if n[:2] == "fx"] + [128])
+        rows_of = lambda d: {"2": (0, cut), "x": (cut, 128)}.get(d, (0, 128))
+        key = lambda d, b=0, step=1, rows=None: A(LISTS[d][1], LISTS[d][2] + b, LISTS[d][2] + 128, step, rows or rows_of(d))
+        bank_of = {n[1:4]: args(n)[2] for n in names if n[0] == "w" and n != "ws"}
+        sums = lambda d: [n for n in order["P"] if n[0] == "p" and args(n)[0] == d]
+        folds = lambda d: [n for n in order["G"] if n[:2] == "f" + d]
 
-        def key_start(d):
-            kind, code, bank = LISTS[d]
-            block = 128 if kind == "S" else 0
+        def task(e, n, free):
+            d = args(n)[0]
+            if n[0] == "g":
+                lo, hi = span(n, 256)
+                off = A("cu", 128 * int(d) + lo // 16, 128 * int(d) + hi // 16)
+                if d in raw:
+                    return 2.7 * (hi - lo) / V, [], lambda: gather(e, A(raw[d], lo, hi), z, off)
+                return (2.7 * (hi - lo) / V, sums({"4": "6", "1": "5"}.get(d)) + [wish(hi)],
+                        lambda: gtt(A(mbuf[d], lo, hi), z, off, A("w", lo, hi), ALU.min))
+            if n == "ws":
+                def wsum():
+                    for b in range(16):
+                        mm(A("k3", b, 128, 16), A("w", b, V, 16), A("rw", 8, 16), True, True)
+                free["k3"] = ["t"]
+                return 0.43, ["w2"], wsum
+            if n == "t":
+                return 0.11, ["ws"], lambda: ts(A("wt16"), A("k3", 0, 128), 1.0 / 8192, -2048.0, ALU.mult, ALU.add)
+            if n[0] in "wzr":
+                lo = 512 * int(args(n)[1])
+                bank = A(bank_of[n[1:4]])
+                if n[0] == "w":
+                    needs, free[bank[1]] = free.get(bank[1], []), ["r" + n[1:4]]
+                    return 0.21, needs + [wish(lo + 512)], lambda: mm(bank, eye, A("w", lo, lo + 512), True, False)
+                if n[0] == "z":
+                    return 0.21, gathers(d, lo, lo + 512), lambda: mm(bank, neye, A(raw[d], lo, lo + 512), False, True)
+                out = X(T.xw[:, lo // 256:lo // 256 + 2, :, :], lo // 128, lo // 128 + 4) if d == "3" else A(mbuf[d], lo, lo + 512)
+                if e == "S":
+                    return 0.49, ["z" + n[1:]], lambda: act(out, bank, ACT.Relu)
+                return 0.43, ["z" + n[1:]], lambda: ts(out, bank, 0.0, None, ALU.max)
+            if n[0] == "k":
+                def start():
+                    code, bank, col = LISTS[d.replace("x", "0")]
+                    at = 512 * int(bank[1]) + col
+                    r0, r1 = rows_of(d)
+                    mm(key(d), A("one", r0, r1, rows=(0, 2)), A("cb", at, at + 128, rows=(0, 2)), True, False)
+                    if d == "o":
+                        mm(key(d), eye, A("a16"), False, False)
+                    else:
+                        at = 128 * int(d.replace("x", "2"))
+                        mm(key(d), A("cp16" if d in "0x" else "c16", at + r0, at + r1), eye, False, False,
+                           pre={"00": ("pc", from_partner), "x1": ("py", from_partner)}.get(d + str(t)))
+                    if clipped(d, 0):
+                        mm(key(d), A("nw", r0, r1), A("wt16"), False, False)
+                return 0.1, ["t"] if clipped(d, 0) and t == 0 else [], start
+            if n[0] == "p":
+                lo, hi = span(n, 512)
+                wts = A("rw", 8, 16) if clipped(d, lo) else A("rw", 0, 8)
+                pre = ("p%s%d" % (d.replace("0", "e"), t), len(folds(d)) * from_partner) if folds(d) else None
 
-            def f():
-                mm(key(d), A("one", 0, 128, rows=(0, code + 5)), A("cb", block, block + 128, rows=(0, code + 5)), True, False)
-                if d == "own":
-                    mm(key(d), A("i16"), A("a16"), False, False)
+                def total():
+                    for b in range(16):
+                        m = X(T.xw[:, :, :, b]) if d == "3" else A(mbuf[d], lo + b, hi, 16)
+                        mm(key(d, b, 16, (lo // 16, hi // 16)), m, wts, False, b == 15, pre=pre if b == 0 else None)
+                if clipped(d, lo):
+                    needs = ["r%s.%d" % (d, c) for c in range(lo // 512, hi // 512)]
                 else:
-                    slots = A("cp16") if d == 0 else A("c16", 128 * d, 128 * d + 128)
-                    mm(key(d), slots, A("i16"), False, False, pre=("pc", from_partner) if d == 0 and t == 0 else None)
-                if kind == "S":
-                    mm(key(d), A("nw16"), A("wt16"), False, False)
-            return f
+                    needs = folds(d) or gathers(d, lo, hi)
+                return 0.43 if hi - lo > 512 else 0.22, needs, total
+            if n == "mE":
+                return 0.22, ["s"], lambda: tt(bk, bk, rin, ALU.min, pre=("pr%d" % t, from_partner))
+            if n[0] == "m":
+                if d in "6o":
+                    return 0.17, sums(d), lambda: act(A("bf" if d == "6" else "rf"), key(d), ACT.Copy)
+                out, in0, needs = {"5": (bk, A("bf"), ["m6"]), "0": (rk, A("rf"), ["mo"])}.get(d, (bk, bk, []))
+                if d in "2x":
+                    out = in0 = A(rk[1] if d == "x" else "bk", rows=rows_of(d))
+                return 0.11, sums(d) + needs, lambda: tt(out, in0, key(d), ALU.min)
+            if n[0] == "a":
+                buf, bits = (rk, 4096) if d == "r" else (bk, 6144)
+                return 0.11, [], lambda: ts(buf, buf, -1 - bits, None, ALU.bitwise_and)
+            if n == "c":
+                return 0.8, [], later_constants
+            if n == "y":
+                return 0.1, [], lambda: send(partner, A("cp16", 256, 384), [A("c16", 256, 384)], "py")
+            if n == "fo":
+                return 0.1, ["w2"], lambda: send(partner, A(mbuf["o"]), [z, A("w")], "po%d" % t), 3.5
+            if n[0] == "f":
+                lo, hi = span(n, 256)
+                return (0.1, gathers(d.replace("x", "2"), lo, hi) + [wish(hi)],
+                        lambda: send(partner, A(mbuf[d], lo, hi), [A(raw[d], lo, hi), A("w", lo, hi)],
+                                     "p%s%d" % (d.replace("0", "e"), t)), 3.5)
+            if n == "s":
+                return 0.1, ["mx" if cut < 128 else "ar"], lambda: send(partner, rin, [rk], "pr%d" % t), 1.5
+            return 1.3, [], lambda: iota(A("jj", 0, HV * NB), [[0, HV], [1, NB]], 0, 0)
 
-        def key_sum(d, lo, hi):
-            kind, code, bank = LISTS[d]
-            wts = A("rw", 8, 16) if kind == "S" else A("rw", 0, 8)
-            pre = ("po%d" % t, from_partner) if d == "own" else ("pe%d" % t, 2 * from_partner) if d == 0 else None
-
-            def f():
-                for b in range(16):
-                    m = X(T.xw[:, :, :, b]) if d == 3 else A(mbuf[d], lo + b, hi, 16)
-                    mm(A(bank, b, 128, 16, rows=(lo // 16, hi // 16)), m, wts, False, b == 15, pre=pre if b == 0 else None)
-            return f
-
-        def merge(d, out, in0, needs=()):
-            return (MERGE, ["key%s" % d] + list(needs), lambda: tt(out, in0, key(d), ALU.min), "mg%s" % d)
-
-        def first(d, out):
-            return (0.17, ["key%s" % d], lambda: act(out, key(d), ACT.Copy), "mg%s" % d)
-
-        def clear(buf, bits, name):
-            return (MERGE, [], lambda: ts(buf, buf, -1 - bits, None, ALU.bitwise_and), name)
-
-        def vgather(d, lo, hi, needs=()):
-            return (GV * (hi - lo) / V, [part(hi - 1)] + list(needs),
-                    lambda: gtt(A(mbuf[d], lo, hi), z, offs(d, lo, hi), A("w", lo, hi), ALU.min), "m%d_%d" % (d, hi))
-
-        own = (0.1, ["w2"], lambda: send(partner, A(mbuf["own"]), [z, A("w")], "po%d" % t), "own_in", 3.5)
-        for k in range(2):
-            lo = 1024 * k
-            sq.append((GS, [], (lambda lo=lo: gather("S", A(ze, lo, lo + 1024), z, offs(0, lo, lo + 1024))), "eg%d" % k))
-            gq.append((0.1, ["eg%d" % k, "w%d" % (k + 1)],
-                       (lambda lo=lo: send(partner, A(mbuf[0], lo, lo + 1024), [A(ze, lo, lo + 1024), A("w", lo, lo + 1024)], "pe%d" % t)),
-                       "e_in%d" % k, 4.0))
-        gq.insert(1 - t, own)
-        if t == 0:
-            gq.append((1.3, [], lambda: iota(A("jj", 0, HV * NB), [[0, HV], [1, NB]], 0, 0), "jj"))
-        gq.append((0.1, ["rclear"], lambda: send(partner, rin, [rk], "pr%d" % t), "r_in", 1.5))
-        clipped = {3: [], 2: []}
-        pend = []
-        for k in range(4):
-            d, lo, zc = (3, 2)[k // 2], 1024 * (k % 2), 1024 * (k % 3)
-            sq.append((GS, [],
-                       (lambda d=d, lo=lo, zc=zc: gather("S", A("zc", zc, zc + 1024), z, offs(d, lo, lo + 1024))), "sg%d" % k))
-            sq.extend(pend)
-            if k == 1:
-                sq.append(first(6, A("bf")))
-            if k == 2:
-                sq.append(first("own", A("rf")))
-            pend = []
-            for j in range(2):
-                n = 2 * k + j
-                bank, c0, src = A("d%d" % (n % 2)), lo + 512 * j, A("zc", zc + 512 * j, zc + 512 * j + 512)
-                out = X(T.xw[:, c0 // 256:c0 // 256 + 2, :, :], c0 // 128, c0 // 128 + 4) if d == 3 else A(mbuf[d], c0, c0 + 512)
-
-                def diff(bank=bank, c0=c0, src=src):
-                    mm(bank, eye, A("w", c0, c0 + 512), True, False)
-                    mm(bank, neye, src, False, True)
-                pq.append((0.43, ["sg%d" % k, part(c0)] + (["sr%d" % (n - 2)] if n >= 2 else []), diff, "sd%d" % n))
-                pend.append((RELU, ["sd%d" % n], (lambda out=out, bank=bank: act(out, bank, ACT.Relu)), "sr%d" % n))
-                clipped[d].append("sr%d" % n)
-        sq.extend(pend)
-        bk = A("bk")
-        tail = (2, 1) if t == 0 else (1, 2)
-        if t == 0:
-            def wsum():
-                for b in range(16):
-                    mm(A("k1", b, 128, 16), A("w", b, V, 16), A("rw", 8, 16), True, True)
-            pq.append((0.43, ["w2"], wsum, "wsum"))
-            vq.extend([vgather(6, 0, 512), vgather(6, 512, 1024), vgather(6, 1024, V),
-                       (0.11, ["wsum"], lambda: ts(A("wt16"), A("k1", 0, 128), 1.0 / 8192, -2048.0, ALU.mult, ALU.add), "wt"),
-                       vgather(5, 0, V)])
-        else:
-            vq.extend([vgather(6, 0, V), vgather(5, 0, V)])
-        vq.extend([vgather(4, 0, 1024, ["key6"]), merge(5, bk, A("bf"), ["mg6"]), vgather(4, 1024, V),
-                   vgather(1, 0, 768), merge(0, rk, A("rf"), ["mgown"]), merge(4, bk, bk), clear(rk, 4096, "rclear"),
-                   vgather(1, 768, TAIL), merge(3, bk, bk),
-                   vgather(1, TAIL, V), clear(bk, 6144, "clear"),
-                   (2 * MERGE, ["r_in"], lambda: tt(bk, bk, rin, ALU.min, pre=("pr%d" % t, from_partner)), "mgr"),
-                   merge(tail[0], bk, bk), merge(tail[1], bk, bk)])
-        ready = {"own": ["own_in", "key5"], 0: ["e_in0", "e_in1", "key4"], 3: clipped[3]}
-        bank_free = {}
-        for d in LISTS:
-            kind, code, bank = LISTS[d]
-            pq.append((0.15, bank_free.get(bank, []) + ["wt"], key_start(d), "ks%s" % d))
-            if d in tail:
-                a, b = (["m1_%d" % TAIL], ["m1_%d" % V]) if d == 1 else (clipped[2][:3], clipped[2][3:])
-                pq.append((0.43, ["ks%s" % d] + a, key_sum(d, 0, TAIL), "part%s" % d))
-                pq.append((0.22, ["part%s" % d] + b + (["key%d" % tail[0]] if d == tail[1] else []), key_sum(d, TAIL, V), "key%s" % d))
-            else:
-                pq.append((0.43, ["ks%s" % d] + ready.get(d, ["m%s_%d" % (d, V)]), key_sum(d, 0, V), "key%s" % d))
-            bank_free[bank] = ["mg%s" % d]
-        for emit in arrange({"V": vq, "S": sq, "G": gq}, pq, known):
+        free = {}
+        tasks = {e: [(n,) + task(e, n, free) for n in order[e]] for e in order}
+        tasks = {e: [x[:2] + (x[2] + after[x[0]],) + x[3:] for x in tasks[e]] for e in tasks}
+        for emit in arrange(tasks, LANDED if t == 0 else dict.fromkeys(LANDED, 0.0)):
             emit()
 
     def trade_and_hand_on(t, zname, zn):
@@ -336,6 +321,8 @@ def rank_program(g, core, T, topo):
         copy(X(T.xw[:, :, 0, :], 0, 1), A("hl", 0, 128))
         copy(X(T.xw[:, :, 1, :], 1, 2), A("hl", 128, 256))
         copy(A("hlb"), A("hl"))
+        if t == 0:
+            tt(A("zz", 144 + 15, 144 + 128, 16), A("i16x", 0, 128, 16), A("eye", 1, 128, 16), ALU.add)
         b = 0
         for bank, eng, n in WINDOW:
             if bank == "d1":
@@ -356,10 +343,10 @@ def rank_program(g, core, T, topo):
         plain(A("k2", 0, 128), True)
         dd = A("k1", 0, 128)
         plain(dd, False)
-        mm(dd, A("a16"), A("ni16"), False, True)
-        gather("S", A("f1", 960, V), A("win"), A("off", 128 + 60, 256))
-        gather("V", A("f1", 0, 960), A("win"), A("off", 128, 128 + 60))
+        mm(dd, A("a16"), neye, False, True)
         copy(A("off", 0, 128), A("k2", 0, 128))
+        gather("S", A("f1", 1024, V), A("win"), A("off", 192, 256))
+        gather("V", A("f1", 0, 1024), A("win"), A("off", 128, 192))
         mm(A("d0", 0, NB), bo, A("zo", 0, NB), True, False)
         mm(A("d1", 0, NB), A("nst"), A("zo", 0, NB), True, False)
         plain(A("k0", 0, 128), False)
@@ -372,20 +359,22 @@ def rank_program(g, core, T, topo):
         gather("S", A(zname, V, V + 128), z, A("off", 0, 8))
         tt(A("ex"), A("k2", 0, 128), A("at"), ALU.is_equal)
         tt(A("zx"), A("ex"), dd, ALU.mult)
-        mm(A("k3", 0, 128), A("ni16"), A("zx"), False, True)
+        mm(A("k3", 0, 128), neye, A("zx"), False, True)
         tt(A("u"), A("k3", 0, 128), A("at"), ALU.not_equal)
         mm(A("d0", 0, 128), bo, A("u"), False, False)
         mm(A("d0", 128, NB), A("nbo"), A("u", 0, 8), False, True)
+        tt(A("tm"), A("u"), dd, ALU.mult)
         mm(A("d1", 0, 128), A("nst"), A("u"), False, False)
         mm(A("d1", 128, NB), A("st"), A("u", 0, 8), False, True)
-        tt(A("tm"), A("u"), dd, ALU.mult)
-        mm(A("k0", 0, 128), A("ni16"), A("tm"), False, True)
+        mm(A("k0", 0, 128), neye, A("tm"), False, True)
         cum = A("cum", 0, NB)
         scan(cum, A("d0", 0, NB), A("one", 0, NB), ALU.add, ALU.mult)
         for h in range(HV, 8):
             jk, kc, cn = A("junk", NB * h, NB * h + NB), A("kc", h, h + 1), A("cnt", h, h + 1)
             op("S", lambda q, jk=jk, kc=kc, cn=cn: q.activation(jk[0], cum[0], ACT.Sign, bias=kc[0], scale=-1.0, accum_out=cn[0]),
                [cum, kc], [jk, cn])
+        copy(A("offg"), A("k0", 0, 128))
+        gather("S", A(zn, TRADE_SPLIT, V), z, A("offg", TRADE_SPLIT // 16, 128))
         for h in range(HV):
             ts(A("le", NB * h, NB * h + NB), cum, A("kb", h, h + 1), None, ALU.is_le)
         tt(A("pp", 0, NB), A("d1", 0, NB), cum, ALU.add)
@@ -394,11 +383,9 @@ def rank_program(g, core, T, topo):
         copy(A("offc", 0, HV), A("sc", NB - 1, HV * NB, NB))
         gtt(A("oh"), A("pp", 0, NB), A("offc"), A("jj", 0, 128), ALU.is_le)
         copy(A("cbf"), A("offc"))
-        copy(A("offg"), A("k0", 0, 128))
         for j in range(16):
             mm(A("k2", 0, 8), A("zz", 15 - j, 143 - j), A("oh", j, 128, 16), j == 0, False)
         mm(A("k2", 0, 8), A("i16x"), A("cbf"), False, True)
-        gather("S", A(zn, TRADE_SPLIT, V), z, A("offg", TRADE_SPLIT // 16, 128))
         copy(A("offt"), A("k2", 0, 8))
         out, land = A("out%d" % t), A("land%d" % t)
         gather("V", out, A(zname), A("offt"))

from concourse.bass import DstId, RemoteDMATransfer
from concourse.mybir import AluOpType as ALU, ActivationFunctionType as ACT

V = 2048
NB = 136
HV = 5
ROUNDS = 2
TRADE_SPLIT = 384
BF, F32, I32, U16, F16 = "bfloat16", "float32", "int32", "uint16", "float16"

SCRATCH = {}
for _dt, _bufs in (
        (BF, "z0 2176 z1 2176 w 2048 mv0 2048 mv1 2048 ms 2048 zc2 2048 zc3 2048 ze0 2048 ze1 2048 eo0 2048 eo1 2048 ex1 2048 "
             "ee0 2048 ee1 2048 hlb 256 win 2048 f1 2048 f2 2048 one 144 eye 128 neye 128 nw 128 i16x 128 i128x 128 "
             "bo 128 nbo 128 st 128 nst 128 rw 16 zz 288 cb 1024 zo 144 jj 688 ex 128 u 128 cum 144 junk 1088 le 688 "
             "sc 688 kb 8 pp 144 oh 128 cbf 8 out0 128 out1 128 land0 128 land1 128"),
        (F16, "c16 896 cp16 384 a16 128 wt16 128 zx 128 tm 128"),
        (F32, "aturn 128 at 128 kc 8 bf 128 rf 128 cnt 8"),
        (I32, "ci 896 hl 256 bk 128 rk0 128 rk1 128 rin0 128 rin1 128 oi 16"),
        (U16, "cu 896 off 256 offc 8 offt 8 offo 8 offg 128")):
    _w = _bufs.split()
    for _k in range(0, len(_w), 2):
        SCRATCH[_w[_k]] = ("sbuf", [128, int(_w[_k + 1])], _dt)
SCRATCH["xw"] = ("sbuf", [128, 8, 16, 16], BF)
PSUM = ["d0", "d1", "k0", "k1", "k2", "k3", "b0", "b1"]
for _k in PSUM:
    SCRATCH[_k] = ("psum", [128, 1024], BF) if _k[0] == "b" else ("psum", [128, 512], F32)

LEFT = ["l%d" % _k for _k in range(12)]
SEMAPHORES = ["eV", "eS", "eP", "eG", "ldc", "ldz", "ldw0", "ldw1", "ldw2", "st", "arr0", "arr1",
              "pc", "po0", "po1", "pe0", "pe1", "px1", "py", "pr0", "pr1"] + LEFT

LISTS = {"6": (3, "k0", 0), "o": (-3, "k0", 128), "4": (1, "k0", 256), "1": (-2, "k0", 384),
         "5": (2, "k1", 0), "0": (-1, "k1", 128), "2": (-1, "k1", 256), "3": (0, "k1", 384), "x": (-1, "k0", 0)}
ORDER = [
    {"V": "g0.7.8 g6.0.2 g6.2.5 g6.5.8 t g5.0.8 g4.0.4 m5 g4.4.8 g1.0.4 m4 m0 m3 ar g1.4.6 ab g1.6.8 mE m2 m1",
     "S": "g0.0.4 g0.4.7 g3.0.4 g3.4.8 r3.0 r3.1 m6 g2.0.4 r3.2 r3.3 g2.4.8 mo r2.0 r2.1 r2.2 r2.3 c",
     "P": "k6 k5 w3.0.d0 w3.1.d1 ws w3.2.k2 z3.0 z3.1 p6.0.4 ko w3.3.k3 z3.2 z3.3 w2.0.d0 w2.1.d1 p5.0.4 k3 z2.0 z2.1 "
          "po.0.4 k4 p3.0.4 k0 p4.0.4 p0.0.4 w2.2.k2 w2.3.k3 z2.2 z2.3 k1 k2 p1.0.3 p2.0.4 p1.3.4",
     "G": "f0.0.4 fo f0.4.8 j s y"},
    {"V": "g6.0.8 g5.0.8 g4.0.4 m5 g4.4.8 g1.0.4 m0 m4 ar mx g1.4.6 m3 g1.6.7 ab g1.7.8 mE m2 m1",
     "S": "g0.0.8 g2.4.8 m6 g3.0.4 g3.4.8 r3.0 r3.1 mo g2.0.2 r3.2 r3.3 g2.2.4 r2.0 r2.1",
     "P": "k6 k5 w3.0.d0 w3.1.d1 w3.2.k2 w3.3.k3 p6.0.4 ko p5.0.4 k0 z3.0 z3.1 po.0.4 k4 z3.2 z3.3 p0.0.4 k3 p4.0.4 "
          "kx w2.0.d0 px.2.4 z2.0 w2.1.d1 p3.0.4<m0 k1<mx z2.1 p1.0.3 k2 p2.0.1 p2.1.2 p1.3.4",
     "G": "fo f0.0.8 fx.4.8 s"}]
WISH = (0, 512, 1280, V)
LANDED = {"w0": 0.5, "w1": 0.9, "w2": 1.8}
WINDOW = (("d0", "S", 3), ("b0", "V", 4), ("b1", "V", 4), ("d1", "S", 2), ("b0", "V", 3))


def arrange(queues, known):
    done, clock, pos, out = dict(known), dict.fromkeys(queues, 0.0), dict.fromkeys(queues, 0), []
    while any(pos[e] < len(queues[e]) for e in queues):
        heads = [(e, queues[e][pos[e]]) for e in queues if pos[e] < len(queues[e])]
        start, e, t = min([(max([clock[e]] + [done[n] for n in t[2]]), e, t) for e, t in heads if all(n in done for n in t[2])],
                          key=lambda c: c[:2])
        pos[e] += 1
        clock[e] = start + t[1]
        done[t[0]] = clock[e] + (t[4] if len(t) > 4 else 0.1)
        out.append(t[3])
    return out


def rank_program(g, core, T, topo):
    rank = T.rank_of(core)
    if rank is None:
        return
    n_ranks = len(T.cores)
    by_die = sorted(T.cores, key=lambda c: (topo.chip(c), topo.die(c), c))
    place = by_die.index(core)
    partner = by_die[place + 1 if place % 2 == 0 else place - 1]
    queue = {"V": g.vector, "S": g.scalar, "P": g.tensor, "G": g, "Y": g.sync}
    ops, left = [], []

    def A(name, lo=0, hi=None, step=1, rows=None):
        hi = SCRATCH[name][1][1] if hi is None else hi
        r = slice(0, 128) if rows is None else slice(rows[0], rows[1])
        ap = T[name][r, lo:hi:step] if step > 1 else T[name][r, lo:hi]
        return (ap, name, lo, hi)

    def X(ap, lo=0, hi=16):
        return (ap, "xw", lo, hi)

    def op(eng, fn, reads, writes, sem=None, pre=None):
        ops.append({"eng": eng, "fn": fn, "r": [a[1:] for a in reads], "w": [a[1:] for a in writes], "sem": sem, "pre": pre})

    def ind(win, off):
        return win[0].indirect(off[0])

    def mm(out, lhs, rhs, start, stop, pre=None):
        op("P", lambda q: q.matmul(out[0], lhs[0], rhs[0], start, stop), [lhs, rhs], [out], pre=pre)

    def copy(out, in_):
        op("V", lambda q: q.tensor_copy(out[0], in_[0]), [in_], [out])

    def tt(out, a, b, alu, pre=None):
        op("V", lambda q: q.tensor_tensor(out[0], a[0], b[0], alu), [a, b], [out], pre=pre)

    def ts(out, a, s1, s2, op0, op1=None):
        rd = [a] + [s for s in (s1, s2) if isinstance(s, tuple)]
        v1 = s1[0] if isinstance(s1, tuple) else s1
        if op1 is None:
            op("V", lambda q: q.tensor_scalar(out[0], a[0], v1, None, op0), rd, [out])
        else:
            op("V", lambda q: q.tensor_scalar(out[0], a[0], v1, s2, op0, op1), rd, [out])

    def scan(out, d0, d1, op0, op1):
        op("V", lambda q: q.tensor_tensor_scan(out[0], d0[0], d1[0], 0.0, op0, op1), [d0, d1], [out])

    def gtt(out, win, off, b, alu):
        op("V", lambda q: q.tensor_tensor(out[0], ind(win, off), b[0], alu), [win, off, b], [out])

    def gather(eng, out, win, off):
        if eng == "V":
            op("V", lambda q: q.tensor_copy(out[0], ind(win, off)), [win, off], [out])
        else:
            op("S", lambda q: q.activation(out[0], ind(win, off), ACT.Copy), [win, off], [out])

    def act(out, in_, func, scale=1.0):
        op("S", lambda q: q.activation(out[0], in_[0], func, scale=scale), [in_], [out])

    def memset(out, val):
        op("V", lambda q: q.memset(out[0], val), [], [out])

    def iota(out, pattern, base, mult):
        op("G", lambda q: q.iota(out[0], pattern, base, mult, allow_small_or_imprecise_dtypes=True), [], [out])

    def select(out, in_, pattern, cmp, base, mult):
        op("G", lambda q: q.affine_select(out[0], in_[0], pattern, cmp, 0.0, base, mult), [in_], [out])

    def load(eng, out, src, sem):
        op(eng, lambda q: q.dma_start(out[0], src), [], [out], sem=(sem, 16))

    def send(dst, land, srcs, sem):
        rid, pid, _ = topo.addr(dst)
        mask = topo.mask(core, dst)
        loc = LEFT[len(left)]
        left.append((loc, len(topo.engines(core, dst))))
        if len(srcs) == 1:
            fn = lambda q: q.remote_dma(land[0], srcs[0][0], T.sem[sem], T.sem[loc], pid, rid, mask)
        else:
            fn = lambda q: q.remote_dma_fused(
                [RemoteDMATransfer(dst_ids=[DstId(rid=rid, pnc=pid)], dma_engine_mask=mask, remote_sem=T.sem[sem],
                                   srcs=[s[0] for s in srcs], dsts=[land[0]], alu_op=3)], local_sem=T.sem[loc])
        op("G", fn, srcs, [], sem=left[-1] + ("remote",))

    def lists_in(lo, hi):
        copy(A("cu", 128 * lo, 128 * hi), A("ci", 128 * lo, 128 * hi))

    def lists_half(lo, hi):
        copy(A("c16", 128 * lo, 128 * hi), A("cu", 128 * lo, 128 * hi))

    eye, neye, bo, one = A("eye"), A("neye"), A("bo"), A("one", 0, 128)
    from_partner = len(topo.engines(partner, core))

    load("Y", A("ci"), T.cand[:], "ldc")
    load("Y", A("z0", 0, V), T.goods[:], "ldz")
    for k in range(3):
        load("Y", A("w", WISH[k], WISH[k + 1]), T.wish[:, WISH[k]:WISH[k + 1]], "ldw%d" % k)

    memset(A("one"), 1.0)
    select(eye, one, [[-1, 128]], ALU.is_equal, 0, 1)
    iota(A("aturn"), [[0, 8], [1, 16]], 0, 16)
    select(bo, one, [[-16, 8], [0, 16]], ALU.is_ge, 0, 1)
    select(bo, bo, [[16, 8], [0, 16]], ALU.is_ge, 15, -1)
    select(A("st"), bo, [[-1, 128]], ALU.is_gt, 0, 1)
    for code, bank, col in [LISTS[d] for d in "o0123456"]:
        at = 512 * int(bank[1]) + col
        memset(A("cb", at, at + 128, rows=(0, 2)), 2048.0 * code - 8192.0)
    memset(A("zz"), 0.0)
    memset(A("cb", 0, 768, rows=(0, 1)), float(1 << 24))
    memset(A("cb", 768, 1024, rows=(0, 1)), 0.0)
    memset(A("zo", 0, 128), 0.0)
    memset(A("zo", 128, 144), 1.0)
    copy(A("a16"), A("aturn"))
    act(neye, eye, ACT.Copy, -1.0)
    act(A("nw"), eye, ACT.Copy, -8192.0)
    mm(A("k3", 0, 128), A("a16"), eye, True, True)
    act(A("at"), A("k3", 0, 128), ACT.Copy)
    act(A("rw", 0, 8), A("bo", 0, 128, 16), ACT.Copy, -8192.0)
    act(A("rw", 8, 16), A("bo", 0, 128, 16), ACT.Copy, 8192.0)
    lists_in(0, 1)
    lists_in(1, 7)
    lists_half(0, 1)
    send(partner, A("cp16", 0, 128), [A("c16", 0, 128)], "pc")
    lists_half(1, 7)

    def later_constants():
        act(A("i16x"), eye, ACT.Copy, 16.0)
        act(A("i128x"), eye, ACT.Copy, 128.0)
        act(A("nbo"), bo, ACT.Copy, -1.0)
        act(A("nst"), A("st"), ACT.Copy, -1.0)
        act(A("zz", 15, 128, 16), A("bo", 0, 128, 16), ACT.Copy)
        act(A("kb"), A("at", 0, 8), ACT.Copy)
        op("S", lambda q: q.activation(T.kc[:], T.at[:, 0:8], ACT.Identity, bias=0.5), [A("at")], [A("kc")])

    def pointers(t, z):
        z = A(z, 0, V)
        after = {n.split("<")[0]: n.split("<")[1:] for e in "VSPG" for n in ORDER[t][e].split()}
        order = {e: [n.split("<")[0] for n in ORDER[t][e].split()] for e in "VSPG"}
        names = [n for e in order for n in order[e]]
        args = lambda n: n[1:].split(".")
        span = lambda n, unit: (unit * int(args(n)[1]), unit * int(args(n)[2]))
        gathers = lambda d, lo, hi: [n for n in names if n[:2] == "g" + d and span(n, 256)[0] < hi and lo < span(n, 256)[1]]
        clipped = lambda d, col: "r%s.%d" % (d, col // 512) in names
        wish = lambda hi: "w%d" % ((hi > WISH[1]) + (hi > WISH[2]))
        mbuf = {"6": "mv0", "5": "mv1", "4": "mv0", "1": "mv1", "2": "ms", "o": "eo%d" % t, "0": "ee%d" % t, "x": "ex%d" % t}
        raw = {"0": "ze%d" % t, "3": "zc3", "2": "zc2", "x": "zc2"}
        bk, rk, rin = A("bk"), A("rk%d" % t), A("rin%d" % t)
        cut = min([span(n, 256)[0] // 16 for n in order["G"] if n[:2] == "fx"] + [128])
        rows_of = lambda d: {"2": (0, cut), "x": (cut, 128)}.get(d, (0, 128))
        key = lambda d, b=0, step=1, rows=None: A(LISTS[d][1], LISTS[d][2] + b, LISTS[d][2] + 128, step, rows or rows_of(d))
        bank_of = {n[1:4]: args(n)[2] for n in names if n[0] == "w" and n != "ws"}
        sums = lambda d: [n for n in order["P"] if n[0] == "p" and args(n)[0] == d]
        folds = lambda d: [n for n in order["G"] if n[:2] == "f" + d]

        def task(e, n, free):
            d = args(n)[0]
            if n[0] == "g":
                lo, hi = span(n, 256)
                off = A("cu", 128 * int(d) + lo // 16, 128 * int(d) + hi // 16)
                if d in raw:
                    return 2.7 * (hi - lo) / V, [], lambda: gather(e, A(raw[d], lo, hi), z, off)
                return (2.7 * (hi - lo) / V, sums({"4": "6", "1": "5"}.get(d)) + [wish(hi)],
                        lambda: gtt(A(mbuf[d], lo, hi), z, off, A("w", lo, hi), ALU.min))
            if n == "ws":
                def wsum():
                    for b in range(16):
                        mm(A("k3", b, 128, 16), A("w", b, V, 16), A("rw", 8, 16), True, True)
                free["k3"] = ["t"]
                return 0.43, ["w2"], wsum
            if n == "t":
                return 0.11, ["ws"], lambda: ts(A("wt16"), A("k3", 0, 128), 1.0 / 8192, -2048.0, ALU.mult, ALU.add)
            if n[0] in "wzr":
                lo = 512 * int(args(n)[1])
                bank = A(bank_of[n[1:4]])
                if n[0] == "w":
                    needs, free[bank[1]] = free.get(bank[1], []), ["r" + n[1:4]]
                    return 0.21, needs + [wish(lo + 512)], lambda: mm(bank, eye, A("w", lo, lo + 512), True, False)
                if n[0] == "z":
                    return 0.21, gathers(d, lo, lo + 512), lambda: mm(bank, neye, A(raw[d], lo, lo + 512), False, True)
                out = X(T.xw[:, lo // 256:lo // 256 + 2, :, :], lo // 128, lo // 128 + 4) if d == "3" else A(mbuf[d], lo, lo + 512)
                if e == "S":
                    return 0.49, ["z" + n[1:]], lambda: act(out, bank, ACT.Relu)
                return 0.43, ["z" + n[1:]], lambda: ts(out, bank, 0.0, None, ALU.max)
            if n[0] == "k":
                def start():
                    code, bank, col = LISTS[d.replace("x", "0")]
                    at = 512 * int(bank[1]) + col
                    r0, r1 = rows_of(d)
                    mm(key(d), A("one", r0, r1, rows=(0, 2)), A("cb", at, at + 128, rows=(0, 2)), True, False)
                    if d == "o":
                        mm(key(d), eye, A("a16"), False, False)
                    else:
                        at = 128 * int(d.replace("x", "2"))
                        mm(key(d), A("cp16" if d in "0x" else "c16", at + r0, at + r1), eye, False, False,
                           pre={"00": ("pc", from_partner), "x1": ("py", from_partner)}.get(d + str(t)))
                    if clipped(d, 0):
                        mm(key(d), A("nw", r0, r1), A("wt16"), False, False)
                return 0.1, ["t"] if clipped(d, 0) and t == 0 else [], start
            if n[0] == "p":
                lo, hi = span(n, 512)
                wts = A("rw", 8, 16) if clipped(d, lo) else A("rw", 0, 8)
                pre = ("p%s%d" % (d.replace("0", "e"), t), len(folds(d)) * from_partner) if folds(d) else None

                def total():
                    for b in range(16):
                        m = X(T.xw[:, :, :, b]) if d == "3" else A(mbuf[d], lo + b, hi, 16)
                        mm(key(d, b, 16, (lo // 16, hi // 16)), m, wts, False, b == 15, pre=pre if b == 0 else None)
                if clipped(d, lo):
                    needs = ["r%s.%d" % (d, c) for c in range(lo // 512, hi // 512)]
                else:
                    needs = folds(d) or gathers(d, lo, hi)
                return 0.43 if hi - lo > 512 else 0.22, needs, total
            if n == "mE":
                return 0.22, ["s"], lambda: tt(bk, bk, rin, ALU.min, pre=("pr%d" % t, from_partner))
            if n[0] == "m":
                if d in "6o":
                    return 0.17, sums(d), lambda: act(A("bf" if d == "6" else "rf"), key(d), ACT.Copy)
                out, in0, needs = {"5": (bk, A("bf"), ["m6"]), "0": (rk, A("rf"), ["mo"])}.get(d, (bk, bk, []))
                if d in "2x":
                    out = in0 = A(rk[1] if d == "x" else "bk", rows=rows_of(d))
                return 0.11, sums(d) + needs, lambda: tt(out, in0, key(d), ALU.min)
            if n[0] == "a":
                buf, bits = (rk, 4096) if d == "r" else (bk, 6144)
                return 0.11, [], lambda: ts(buf, buf, -1 - bits, None, ALU.bitwise_and)
            if n == "c":
                return 0.8, [], later_constants
            if n == "y":
                return 0.1, [], lambda: send(partner, A("cp16", 256, 384), [A("c16", 256, 384)], "py")
            if n == "fo":
                return 0.1, ["w2"], lambda: send(partner, A(mbuf["o"]), [z, A("w")], "po%d" % t), 3.5
            if n[0] == "f":
                lo, hi = span(n, 256)
                return (0.1, gathers(d.replace("x", "2"), lo, hi) + [wish(hi)],
                        lambda: send(partner, A(mbuf[d], lo, hi), [A(raw[d], lo, hi), A("w", lo, hi)],
                                     "p%s%d" % (d.replace("0", "e"), t)), 3.5)
            if n == "s":
                return 0.1, ["mx" if cut < 128 else "ar"], lambda: send(partner, rin, [rk], "pr%d" % t), 1.5
            return 1.3, [], lambda: iota(A("jj", 0, HV * NB), [[0, HV], [1, NB]], 0, 0)

        free = {}
        tasks = {e: [(n,) + task(e, n, free) for n in order[e]] for e in order}
        tasks = {e: [x[:2] + (x[2] + after[x[0]],) + x[3:] for x in tasks[e]] for e in tasks}
        for emit in arrange(tasks, LANDED if t == 0 else dict.fromkeys(LANDED, 0.0)):
            emit()

    def trade_and_hand_on(t, zname, zn):
        z = A(zname, 0, V)
        hi, lo = A("hlb", 0, 128), A("hlb", 128, 256)

        def plain(out, stop):
            mm(out, hi, A("i16x"), True, False)
            mm(out, lo, eye, False, stop)

        def to_list(out, src, c0, c1, start):
            for b in range(16):
                mm(A(out, c0, c1), A("zz", 144 + 15 - b, 144 + 143 - b), A(src, 16 * c0 + b, 16 * c1, 16), start and b == 0, start and b == 15)
        ts(A("hl", 0, 128), A("bk"), 4, 127, ALU.arith_shift_right, ALU.bitwise_and)
        ts(A("hl", 128, 256), A("bk"), 15, None, ALU.bitwise_and)
        copy(X(T.xw[:, :, 0, :], 0, 1), A("hl", 0, 128))
        copy(X(T.xw[:, :, 1, :], 1, 2), A("hl", 128, 256))
        copy(A("hlb"), A("hl"))
        if t == 0:
            tt(A("zz", 144 + 15, 144 + 128, 16), A("i16x", 0, 128, 16), A("eye", 1, 128, 16), ALU.add)
        b = 0
        for bank, eng, n in WINDOW:
            if bank == "d1":
                mm(A("k0", 128, 256), hi, eye, True, False)
                mm(A("k0", 128, 256), lo, A("i128x"), False, True)
                copy(A("off", 128, 256), A("k0", 128, 256))
            for j in range(n):
                src, dst = X(T.xw[:, :, :, b + j]), A(bank, 128 * j, 128 * j + 128)
                if eng == "S":
                    mm(dst, src, eye, True, True)
                else:
                    op("P", lambda q, src=src, dst=dst: q.transpose(dst[0], src[0], eye[0]), [src, eye], [dst])
            if eng == "S":
                act(A("win", 128 * b, 128 * (b + n)), A(bank, 0, 128 * n), ACT.Copy)
            else:
                copy(A("win", 128 * b, 128 * (b + n)), A(bank, 0, 128 * n))
            b += n
        plain(A("k2", 0, 128), True)
        dd = A("k1", 0, 128)
        plain(dd, False)
        mm(dd, A("a16"), neye, False, True)
        copy(A("off", 0, 128), A("k2", 0, 128))
        gather("S", A("f1", 1024, V), A("win"), A("off", 192, 256))
        gather("V", A("f1", 0, 1024), A("win"), A("off", 128, 192))
        mm(A("d0", 0, NB), bo, A("zo", 0, NB), True, False)
        mm(A("d1", 0, NB), A("nst"), A("zo", 0, NB), True, False)
        plain(A("k0", 0, 128), False)
        for k in range(4):
            gather("VS"[k % 2], A("f2", 512 * k, 512 * k + 512), A("f1"), A("off", 32 * k, 32 * k + 32))
        to_list("k2", "f1", 0, 128, True)
        mm(A("k3", 0, 128), eye, A("zo", 0, 128), True, False)
        to_list("k3", "f2", 0, 64, False)
        to_list("k3", "f2", 64, 128, False)
        gather("S", A(zname, V, V + 128), z, A("off", 0, 8))
        tt(A("ex"), A("k2", 0, 128), A("at"), ALU.is_equal)
        tt(A("zx"), A("ex"), dd, ALU.mult)
        mm(A("k3", 0, 128), neye, A("zx"), False, True)
        tt(A("u"), A("k3", 0, 128), A("at"), ALU.not_equal)
        mm(A("d0", 0, 128), bo, A("u"), False, False)
        mm(A("d0", 128, NB), A("nbo"), A("u", 0, 8), False, True)
        tt(A("tm"), A("u"), dd, ALU.mult)
        mm(A("d1", 0, 128), A("nst"), A("u"), False, False)
        mm(A("d1", 128, NB), A("st"), A("u", 0, 8), False, True)
        mm(A("k0", 0, 128), neye, A("tm"), False, True)
        cum = A("cum", 0, NB)
        scan(cum, A("d0", 0, NB), A("one", 0, NB), ALU.add, ALU.mult)
        for h in range(HV, 8):
            jk, kc, cn = A("junk", NB * h, NB * h + NB), A("kc", h, h + 1), A("cnt", h, h + 1)
            op("S", lambda q, jk=jk, kc=kc, cn=cn: q.activation(jk[0], cum[0], ACT.Sign, bias=kc[0], scale=-1.0, accum_out=cn[0]),
               [cum, kc], [jk, cn])
        copy(A("offg"), A("k0", 0, 128))
        gather("S", A(zn, TRADE_SPLIT, V), z, A("offg", TRADE_SPLIT // 16, 128))
        for h in range(HV):
            ts(A("le", NB * h, NB * h + NB), cum, A("kb", h, h + 1), None, ALU.is_le)
        tt(A("pp", 0, NB), A("d1", 0, NB), cum, ALU.add)
        scan(A("sc", 0, HV * NB), A("jj", 0, HV * NB), A("le", 0, HV * NB), ALU.min, ALU.add)
        ts(A("offc", HV, 8), A("cnt", HV, 8), 0.5, NB / 2, ALU.mult, ALU.add)
        copy(A("offc", 0, HV), A("sc", NB - 1, HV * NB, NB))
        gtt(A("oh"), A("pp", 0, NB), A("offc"), A("jj", 0, 128), ALU.is_le)
        copy(A("cbf"), A("offc"))
        for j in range(16):
            mm(A("k2", 0, 8), A("zz", 15 - j, 143 - j), A("oh", j, 128, 16), j == 0, False)
        mm(A("k2", 0, 8), A("i16x"), A("cbf"), False, True)
        copy(A("offt"), A("k2", 0, 8))
        out, land = A("out%d" % t), A("land%d" % t)
        gather("V", out, A(zname), A("offt"))
        send(T.cores[(rank + 1 + t) % n_ranks], land, [out], "arr%d" % t)
        n_in = len(topo.engines(T.cores[(rank - 1 - t) % n_ranks], core))
        copy(A("oi", 0, 8), A("offt"))
        gather("V", A(zn, 0, TRADE_SPLIT), z, A("offg", 0, TRADE_SPLIT // 16))
        ts(A("oi", 8, 16), A("oi", 0, 8), V - 1, None, ALU.bitwise_and)
        copy(A("offo"), A("oi", 8, 16))
        new = A(zn, 0, V)
        op("V", lambda q: q.tensor_copy(ind(new, A("offo")), land[0]), [A("offo"), land], [new], pre=("arr%d" % t, n_in))

    zs = ["z0", "z1"]
    for t in range(ROUNDS):
        pointers(t, zs[t % 2])
        trade_and_hand_on(t, zs[t % 2], zs[(t + 1) % 2])
    last = A(zs[ROUNDS % 2], 0, V)
    op("Y", lambda q: q.dma_start(T.y[:], last[0]), [last], [], sem=("st", 16))

    def meet(a, b):
        return a[0] == b[0] and (a[1] < b[2] and b[1] < a[2])

    name = lambda o: o["sem"][0] if o["sem"] else o["eng"]
    know = {e: {} for e in queue}
    for i, o in enumerate(ops):
        e = o["eng"]
        need = {}
        banks = set(a[0] for a in o["r"] + o["w"] if a[0] in PSUM)
        for j in range(i):
            p = ops[j]
            if p["eng"] == "P" and e == "P":
                continue
            hit = any(meet(a, b) for a in o["r"] + o["w"] for b in p["w"]) or any(meet(a, b) for a in o["w"] for b in p["r"])
            if not hit and banks and p["eng"] != e:
                hit = any(b[0] in banks for b in p["r"] + p["w"])
            if hit:
                need[name(p)] = j
        o["waits"] = []
        for key, j in sorted(need.items(), key=lambda kv: -kv[1]):
            if know[e].get(key, -1) < j:
                o["waits"].append(j)
                ops[j]["inc"] = True
                for k2, v2 in ops[j]["know"].items():
                    know[e][k2] = max(know[e].get(k2, -1), v2)
        o["know"] = dict(know[e])
        o["know"][name(o)] = i
    count = {e: 0 for e in queue}
    for o in ops:
        e = o["eng"]
        q = queue[e]
        for j in o["waits"]:
            q.wait_ge(T.sem[ops[j]["tok"][0]], ops[j]["tok"][1])
        if o["pre"]:
            q.wait_ge(T.sem[o["pre"][0]], o["pre"][1])
        ins = o["fn"](q)
        if o["sem"]:
            o["tok"] = o["sem"][:2]
            if len(o["sem"]) == 2:
                ins.then_inc(T.sem[o["sem"][0]], 16)
        elif o.get("inc"):
            count[e] += 1
            ins.then_inc(T.sem["e" + e], 1)
            o["tok"] = ("e" + e, count[e])
    for loc, n in left:
        g.wait_ge(T.sem[loc], n)
    g.wait_ge(T.sem.st, 16)
